import numpy as np, ml_dtypes
CORES = [48,51,52,55]
N = 4
BF = ml_dtypes.bfloat16
def gentries(a):
    return np.ascontiguousarray(a.reshape(8, 16, -1).transpose(0, 2, 1)).reshape(8, -1)
def gtable(e):
    e = np.asarray(e); return np.ascontiguousarray(e.reshape(8, -1, 16).transpose(0, 2, 1)).reshape(128, -1).astype(np.int32)
M, Q, V, TOP = 2048, 256, 8, 15
WT = 255
def far_maps(rng):
    p = np.argsort(rng.random((N, 8, M)), axis=-1)
    return np.where(rng.random(p.shape) < 0.125, rng.integers(0, M, p.shape), p).astype(np.int32)
def lists(a):
    return np.stack([gtable(u) for u in a])
def setup_inputs(rng):
    return {"nx": far_maps(rng), "w": np.floor((WT + 1) * rng.random((N, 8, M)) ** 32).astype(np.int32), "x": lists(rng.integers(0, M, (N, 8, Q))), "e": lists(rng.integers(0, TOP + 1, (N, 8, V * Q)))}
def setup_inputs_ends(rng):
    d = setup_inputs(rng); k = rng.choice(np.array([0, TOP]), (N, 8, V, Q))
    k[:, :, :, 0] = 0; k[:, :, :, 1] = TOP; k[:, :, :, Q - 1] = 0; k[:, :, V - 1, Q - 1] = TOP
    d["e"] = lists(k.reshape(N, 8, V * Q))
    w = np.where(rng.random((N, 8, M)) < 0.015625, WT, 0); w[:, 0] = WT; d["w"] = w.astype(np.int32)
    return d
def setup_inputs_still(rng):
    d = setup_inputs(rng); a = np.array(d["nx"]); s = int(rng.integers(0, 4)); p = np.arange(M)
    for r in range(N):
        h = (r + s) % 4; c = rng.choice(np.arange(2, M - 1), 8, replace=False)
        if h == 0:
            a[r] = p
        elif h == 1:
            c[0] = 0; c[1] = M - 1; a[r] = rng.permutation(c)[:, None]
        elif h == 2:
            c[0] = 1; c[1] = M - 1; a[r] = (p + rng.permutation(c)[:, None]) % M
        else:
            c[0] = 1; c[1] = M - 1; a[r] = p ^ rng.permutation(c)[:, None]
    d["nx"] = a; return d
def setup_inputs_alike(rng):
    d = setup_inputs(rng); k = rng.integers(0, TOP + 1, (N, 8, V, Q // 2))
    z = np.where((np.arange(N)[:, None] + np.arange(8)) % 2 == 0, M - 1, 0)
    d["x"] = lists(np.repeat(z[:, :, None], Q, axis=2)); d["e"] = lists(np.concatenate([k, k], -1).reshape(N, 8, V * Q)); return d
def setup_inputs_spread(rng):
    d = setup_inputs(rng)
    d["nx"] = np.floor(M * rng.random((N, 8, M)) ** 3).astype(np.int32)
    d["w"] = np.floor((WT + 1) * rng.random((N, 8, M)) ** 16).astype(np.int32)
    d["x"] = lists(np.floor(M * rng.random((N, 8, Q)) ** 2)); d["e"] = lists(np.floor((TOP + 1) * rng.random((N, 8, V * Q)) ** 3)); return d
def check_inputs(d):
    bad = []
    for name, top in (("nx", M - 1), ("w", WT), ("x", M - 1), ("e", TOP)):
        if np.min(d[name]) < 0 or np.max(d[name]) > top: bad.append("range of " + name)
    return bad
def reference(nx, w, x, e):
    last = np.zeros((N, 128, Q // 16), np.int32); peak = np.zeros((N, 128, Q // 16), np.int32); g = np.arange(8)[:, None]
    for r in range(N):
        p = gentries(x[r]).astype(np.int64); k = gentries(e[r]).reshape(8, V, Q); s = np.zeros((8, Q), np.int64)
        for t in range(V):
            q = (r + t) % N
            for i in range(TOP):
                go = i < k[:, t]
                s = np.maximum(s, np.where(go, w[q][g, p], 0))
                p = np.where(go, nx[q][g, p], p)
        last[r] = gtable(p); peak[r] = gtable(s)
    return {"last": np.asarray(last, np.float32), "peak": np.asarray(peak, np.float32)}

@@ -1,0 +1,491 @@
+import numpy as np
+from concourse.bass import DstId, RemoteDMATransfer
+from concourse.mybir import dt, AluOpType, ActivationFunctionType
+
+ND = 40
+SCRATCH = {
+    "srcA": ("dram", [4, 128, 64], "int32"), "srcE": ("dram", [4, 128, 32], "int32"), "srcX": ("dram", [4, 128, 4], "int32"),
+    "landA": ("dram", [4, 128, 64], "int32"), "landE": ("dram", [4, 128, 32], "int32"), "landX": ("dram", [4, 128, 4], "int32"),
+    "landO": ("dram", [4, 128, 32], "float32"),
+    "s2r": ("sbuf", [128, 512], "int32"), "s2f": ("sbuf", [128, 512], "float16"), "l1r": ("sbuf", [128, 128], "int32"),
+    "ep": ("sbuf", [128, 2, 64], "int32"), "ei": ("sbuf", [128, 128], "int32"), "fi": ("sbuf", [128, 128], "int32"), "ki": ("sbuf", [128, 128], "int32"),
+    "fb": ("sbuf", [128, 128], "bfloat16"), "off": ("sbuf", [128, 128], "float16"),
+    "xr": ("sbuf", [128, 16], "int32"), "xa": ("sbuf", [128, 16], "int32"), "xb": ("sbuf", [128, 16], "int32"), "xc": ("sbuf", [128, 16], "int32"), "xd": ("sbuf", [128, 16], "int32"), "xe": ("sbuf", [128, 16], "int32"),
+    "t0": ("sbuf", [128, 2048], "bfloat16"), "t1": ("sbuf", [128, 2048], "bfloat16"), "tab": ("sbuf", [128, 10240], "bfloat16"),
+    "ga": ("sbuf", [128, 2048], "bfloat16"), "gb": ("sbuf", [128, 2048], "bfloat16"), "c4a": ("sbuf", [128, 640], "bfloat16"),
+    "l1": ("sbuf", [128, 128], "uint16"), "l2": ("sbuf", [128, 128], "uint16"), "l4": ("sbuf", [128, 128], "uint16"),
+    "sq": ("sbuf", [128, 2048], "bfloat16"), "em": ("sbuf", [128, 2048], "bfloat16"),
+    "ql0": ("sbuf", [128, 8], "uint16"), "ql1": ("sbuf", [128, 8], "uint16"),
+    "x0": ("sbuf", [128, 128], "bfloat16"), "x1": ("sbuf", [128, 128], "bfloat16"),
+    "y0": ("sbuf", [128, 128], "float16"), "y1": ("sbuf", [128, 128], "float16"),
+    "acc": ("sbuf", [128, 16], "float32"), "yp": ("sbuf", [128, 256], "bfloat16"),
+    "yw0": ("sbuf", [128, 128], "bfloat16"), "yw1": ("sbuf", [128, 128], "bfloat16"),
+    "m05": ("sbuf", [128, 16], "float32"), "m06": ("sbuf", [128, 16], "float32"), "outb": ("sbuf", [128, 32], "float32"),
+    "mi": ("sbuf", [128, 128], "int32"), "kq": ("sbuf", [128, 8], "int32"), "kc": ("sbuf", [128, 8], "int32"), "kf": ("sbuf", [128, 8], "float32"),
+    "ri": ("sbuf", [128, 6, 128], "int32"), "rf": ("sbuf", [128, 7, 128], "bfloat16"),
+    "ro": ("sbuf", [128, 4], "float32"), "rb": ("sbuf", [128, 4], "float32"), "mv": ("sbuf", [128, 4], "float32"),
+    "uu": ("sbuf", [128, 2], "float32"), "cf": ("sbuf", [128, 24], "float32"),
+    "gbd": ("sbuf", [128, 256], "bfloat16"), "dm": ("sbuf", [128, 128], "bfloat16"), "d16": ("sbuf", [128, 16], "float32"),
+    "e16": ("sbuf", [128, 2048], "bfloat16"), "b16": ("sbuf", [128, 16], "float32"),
+    "erw": ("sbuf", [128, 144], "bfloat16"), "gw": ("sbuf", [128, 544], "bfloat16"), "gl": ("sbuf", [128, 512], "bfloat16"),
+    "gb8": ("sbuf", [128, 8], "float16"), "idh": ("sbuf", [128, 128], "float16"),
+    "ka": ("sbuf", [128, 128], "bfloat16"), "kb": ("sbuf", [128, 128], "bfloat16"), "kd": ("sbuf", [128, 128], "bfloat16"), "ke": ("sbuf", [128, 128], "bfloat16"),
+    "lb": ("sbuf", [128, 128], "bfloat16"), "li": ("sbuf", [128, 128], "bfloat16"), "lbv": ("sbuf", [128, 512], "float16"), "liv": ("sbuf", [128, 512], "float16"),
+    "f1": ("sbuf", [128, 128], "bfloat16"), "f2": ("sbuf", [128, 128], "bfloat16"), "f3": ("sbuf", [128, 128], "bfloat16"),
+    "fa": ("sbuf", [128, 128], "bfloat16"), "fra": ("sbuf", [128, 128], "bfloat16"), "frb": ("sbuf", [128, 128], "bfloat16"), "frc": ("sbuf", [128, 128], "bfloat16"), "frd": ("sbuf", [128, 128], "bfloat16"),
+    "fr2": ("sbuf", [128, 128], "bfloat16"), "fr3": ("sbuf", [128, 128], "bfloat16"), "fr4": ("sbuf", [128, 128], "bfloat16"),
+    "g11": ("sbuf", [128, 128], "bfloat16"), "r2a": ("sbuf", [128, 128], "bfloat16"), "r2b": ("sbuf", [128, 128], "bfloat16"), "r2": ("sbuf", [128, 128], "bfloat16"), "r4": ("sbuf", [128, 128], "bfloat16"),
+}
+for _i in range(8):
+    SCRATCH["pb%d" % _i] = ("psum", [128, 512], "float32")
+SEMAPHORES = ["vv", "ss", "pp", "gq", "arrA", "arrE", "arrX", "arrO", "locA", "locE", "locX", "locO"] + ["d%d" % _i for _i in range(ND)]
+
+ADD, SUB, MUL, MAX, EQ = AluOpType.add, AluOpType.subtract, AluOpType.mult, AluOpType.max, AluOpType.is_equal
+AND, SHR = AluOpType.bitwise_and, AluOpType.logical_shift_right
+AF = ActivationFunctionType
+
+
+def rank_program(g, core, T, topo):
+    rank = T.rank_of(core)
+    if rank is None:
+        return
+    queues = {"v": g.vector, "s": g.scalar, "p": g.tensor, "g": g, "y": g.sync}
+    comp = {"v": "vv", "s": "ss", "p": "pp", "g": "gq"}
+    total, known, hist, bank, dmas = {}, {q: {} for q in queues}, {}, {}, [0]
+
+    def wait(q, tok):
+        sem, val, know = tok
+        if known[q].get(sem, 0) < val:
+            queues[q].wait_ge(T.sem[sem], val)
+            known[q][sem] = val
+            for a, b in know.items():
+                if known[q].get(a, 0) < b:
+                    known[q][a] = b
+
+    def deps(q, reads, writes, is_dma):
+        need = []
+        for regs, w in ((reads, False), (writes, True)):
+            for key, lo, hi in regs:
+                if key[:2] == "pb":
+                    for oq, tok in bank.get(key, {}).items():
+                        if oq != q:
+                            need.append(tok)
+                    continue
+                for l, h, tok, oq, ow in hist.get(key, []):
+                    if l < hi and lo < h and (w or ow):
+                        same = oq == q and not is_dma
+                        if same and w:
+                            continue
+                        need.append(tok)
+        best = {}
+        for tok in need:
+            if tok[0] not in best or best[tok[0]][1] < tok[1]:
+                best[tok[0]] = tok
+        toks = list(best.values())
+        for tok in toks:
+            if any(o is not tok and o[2].get(tok[0], 0) >= tok[1] for o in toks):
+                continue
+            wait(q, tok)
+
+    def note(q, tok, reads, writes, is_dma):
+        for regs, w in ((reads, False), (writes, True)):
+            for key, lo, hi in regs:
+                if key[:2] == "pb":
+                    bank.setdefault(key, {})[q] = tok
+                    continue
+                old = hist.setdefault(key, [])
+                if w:
+                    hist[key] = old = [o for o in old if not (lo <= o[0] and o[1] <= hi)]
+                old.append((lo, hi, tok, "dma" if is_dma else q, w))
+
+    def op(q, call, reads, writes):
+        deps(q, reads, writes, False)
+        sem = comp[q]
+        total[sem] = total.get(sem, 0) + 1
+        tok = (sem, total[sem], dict(known[q]))
+        call(queues[q]).then_inc(T.sem[sem], 1)
+        note(q, tok, reads, writes, False)
+        return tok
+
+    def dma(q, out, in_, reads, writes, extra=()):
+        for tok in extra:
+            wait(q, tok)
+        deps(q, reads, writes, True)
+        sem = "d%d" % dmas[0]
+        dmas[0] += 1
+        total[sem] = 16
+        tok = (sem, 16, dict(known[q]))
+        queues[q].dma_start(out, in_).then_inc(T.sem[sem], 16)
+        note(q, tok, reads, writes, True)
+        return tok
+
+    others = [s for s in range(4) if s != rank]
+    SHARE = 4
+
+    def send(src_of, dst, arr, loc, reads):
+        deps("g", reads, [], True)
+        tr = []
+        for i, s in enumerate(others):
+            dstc = T.cores[s]
+            a = topo.addr(dstc)
+            eng = topo.engines(core, dstc)[SHARE * i:SHARE * (i + 1)]
+            tr.append(RemoteDMATransfer(dst_ids=[DstId(rid=a[0], pnc=a[1])], dma_engine_mask=sum(1 << k for k in eng),
+                                        remote_sem=T.sem[arr], src=src_of(s), dst=dst))
+        g.remote_dma_fused(tr, local_sem=T.sem[loc])
+        total[loc] = 3 * SHARE
+        total[arr] = 3 * SHARE
+        return (arr, 3 * SHARE, {})
+
+    def ts(out, in0, s1, s2, *ops):
+        return lambda e: e.tensor_scalar(out, in0, s1, s2, *ops)
+
+    def tt(out, in0, in1, o):
+        return lambda e: e.tensor_tensor(out, in0, in1, o)
+
+    def cp(out, in_):
+        return lambda e: e.tensor_copy(out, in_)
+
+    def act(out, in_, func=AF.Copy, **kw):
+        return lambda e: e.activation(out, in_, func, **kw)
+
+    def mm(out, lhsT, rhs, start=True, stop=True):
+        return lambda e: e.matmul(out, lhsT, rhs, start, stop)
+
+    A3, E3, X3 = T.srcA, T.srcE, T.srcX
+    dma("y", A3[:, 0:64, :], T.nx[:], [], [("srcAn", 0, 1)])
+    dma("s", A3[:, 64:128, :], T.w[:], [], [("srcAw", 0, 1)])
+    dma("y", E3[:], T.e[:], [], [("srcE", 0, 1)])
+    dma("s", X3[:], T.x[:], [], [("srcX", 0, 1)])
+    own = slice(2 * rank, 2 * rank + 2)
+    rows = slice(32 * rank, 32 * rank + 32)
+    dma("y", T.landA[rank, 0:64, :], T.nx[own, :], [], [("landAn", 0, 1)])
+    dma("s", T.landA[rank, 64:128, :], T.w[own, :], [], [("landAw", 0, 1)])
+    dma("y", T.landE[rank], T.e[rows, :], [], [("landE", 0, 1)])
+    dma("s", T.landX[rank], T.x[rows, :], [], [("landX", 0, 1)])
+
+    op("g", lambda e: e.iota(T.kq[:], [[0, 8]], 0, 1), [], [("kq", 0, 8)])
+    op("g", lambda e: e.iota(T.mi[:], [[1, 128]], 0, 0), [], [("mi", 0, 128)])
+    arrA = send(lambda s: A3[s], T.landA[rank], "arrA", "locA", [("srcAn", 0, 1), ("srcAw", 0, 1)])
+    arrE = send(lambda s: E3[s], T.landE[rank], "arrE", "locE", [("srcE", 0, 1)])
+    arrX = send(lambda s: X3[s], T.landX[rank], "arrX", "locX", [("srcX", 0, 1)])
+
+    kf, ro, rb, mv, cf = T.kf, T.ro, T.rb, T.mv, T.cf
+    KQ, KC = T.kq, T.kc
+    for i, (o1, a1, o2, a2) in enumerate([(SHR, 4, None, 0), (AND, 15, None, 0), (AND, 3, None, 0), (SHR, 2, AND, 3),
+                                          (SHR, 5, None, 0), (SHR, 2, AND, 7), (AND, 1, None, 0), (SHR, 1, AND, 1)]):
+        c = ts(KC[:, i:i + 1], KQ[:, i:i + 1], a1, None, o1) if o2 is None else ts(KC[:, i:i + 1], KQ[:, i:i + 1], a1, a2, o1, o2)
+        op("v", c, [("kq", 0, 8)], [("kc", i, i + 1)])
+    op("v", cp(kf[:], KC[:]), [("kc", 0, 8)], [("kf", 0, 8)])
+    for i, (o1, a1, o2, a2) in enumerate([(SHR, 4, None, 0), (AND, 15, None, 0), (SHR, 2, AND, 3), (AND, 1, None, 0), (SHR, 1, AND, 1)]):
+        c = ts(T.ri[:, i, :], T.mi[:], a1, None, o1) if o2 is None else ts(T.ri[:, i, :], T.mi[:], a1, a2, o1, o2)
+        op("v", c, [("mi", 0, 128)], [("ri%d" % i, 0, 128)])
+    op("v", cp(T.rf[:, 5, :], T.mi[:]), [("mi", 0, 128)], [("rf5", 0, 128)])
+    for i in range(5):
+        op("v", cp(T.rf[:, i, :], T.ri[:, i, :]), [("ri%d" % i, 0, 128)], [("rf%d" % i, 0, 128)])
+
+    def R(i):
+        return T.rf[:, i, :]
+
+    def RK(i):
+        return ("rf%d" % i, 0, 128)
+    KF = ("kf", 0, 8)
+
+    def col(i):
+        return cf[:, i:i + 1]
+
+    def ck(i):
+        return ("cf", i, i + 1)
+    W = 128
+    for h in range(2):
+        op("v", ts(T.gbd[:, W * h:W * h + W], R(0), kf[:, 0:1], None, EQ), [RK(0), KF], [("gbd", W * h, W * h + W)])
+    op("v", ts(T.dm[:], R(1), kf[:, 1:2], None, EQ), [RK(1), KF], [("dm", 0, W)])
+    for j in range(4):
+        op("v", ts(ro[:, j:j + 1], kf[:, 3:4], float(j), None, EQ), [KF], [("ro", j, j + 1)])
+        op("v", ts(rb[:, j:j + 1], kf[:, 4:5], float(j), None, EQ), [KF], [("rb", j, j + 1)])
+        op("v", ts(mv[:, j:j + 1], kf[:, 2:3], float(j), None, EQ), [KF], [("mv", j, j + 1)])
+    op("v", cp(T.d16[:], T.dm[:, 0:16]), [("dm", 0, 16)], [("d16", 0, 16)])
+    op("v", ts(T.b16[:], T.rf[:, 5, 0:16], ro[:, 1:2], 1.0, MUL, ADD), [RK(5), ("ro", 1, 2)], [("b16", 0, 16)])
+    GBD, DM = ("gbd", 0, 256), ("dm", 0, W)
+    RO, RB = ("ro", 0, 4), ("rb", 0, 4)
+    op("v", ts(col(0), rb[:, 1:2], 0.0078125, rb[:, 0:1], MUL, ADD), [RB], [ck(0)])
+    op("v", ts(col(2), rb[:, 0:1], -0.0078125, None, MUL), [RB], [ck(2)])
+    op("v", ts(T.kd[:], R(0), kf[:, 5:6], None, EQ), [RK(0), KF], [("kd", 0, W)])
+    op("v", ts(T.f1[:], R(3), 0.0, 512.0, EQ, MUL), [RK(3)], [("f1", 0, W)])
+    op("v", ts(col(1), rb[:, 2:3], 1.0, col(0), MUL, ADD), [RB, ck(0)], [ck(1)])
+    op("v", ts(T.kb[:], R(2), 1.0, col(2), EQ, MUL), [RK(2), ck(2)], [("kb", 0, W)])
+    op("v", ts(T.f2[:], R(2), 2.0, None, EQ), [RK(2)], [("f2", 0, W)])
+    op("v", ts(T.ka[:], R(2), kf[:, 4:5], col(1), EQ, MUL), [RK(2), KF, ck(1)], [("ka", 0, W)])
+    op("v", tt(T.f3[:], T.f2[:], R(3), MUL), [("f2", 0, W), RK(3)], [("f3", 0, W)])
+    op("v", ts(T.ke[:], T.kb[:], rb[:, 3:4], None, ADD), [("kb", 0, W), RB], [("ke", 0, W)])
+    op("v", tt(T.ka[:], T.ka[:], T.ke[:], ADD), [("ka", 0, W), ("ke", 0, W)], [("ka", 0, W)])
+    op("v", tt(T.f1[:], T.f1[:], T.f3[:], ADD), [("f1", 0, W), ("f3", 0, W)], [("f1", 0, W)])
+    op("v", tt(T.lb[:], T.ka[:], T.kd[:], MUL), [("ka", 0, W), ("kd", 0, W)], [("lb", 0, W)])
+    op("v", tt(T.li[:], T.lb[:], T.f1[:], MUL), [("lb", 0, W), ("f1", 0, W)], [("li", 0, W)])
+    for v in range(4):
+        op("v", ts(T.lbv[:, W * v:W * v + W], T.lb[:], mv[:, v:v + 1], None, MUL), [("lb", 0, W), ("mv", v, v + 1)], [("lbv", W * v, W * v + W)])
+    op("v", ts(T.s2f[96:128, 0:128], T.rf[96:128, 5, :], 0.0, 1.0, MUL, ADD), [RK(5)], [("s2k", 0, 128)])
+    for z in range(1, 4):
+        op("v", ts(T.s2f[96:128, W * z:W * z + W], T.rf[96:128, 5, :], 0.0, 1.0, MUL, ADD), [RK(5)], [("s2k", W * z, W * z + W)])
+    for v in range(4):
+        op("v", ts(T.liv[:, W * v:W * v + W], T.li[:], mv[:, v:v + 1], None, MUL), [("li", 0, W), ("mv", v, v + 1)], [("liv", W * v, W * v + W)])
+    op("v", ts(T.uu[:], kf[:, 6:8], 1.0 - 0.001953125, 0.001953125, MUL, ADD), [KF], [("uu", 0, 2)])
+    op("v", ts(col(4), ro[:, 0:1], 16.0, ro[:, 1:2], MUL, ADD), [RO], [ck(4)])
+    op("v", ts(col(6), ro[:, 1:2], 128.0, ro[:, 0:1], MUL, ADD), [RO], [ck(6)])
+    op("v", ts(col(8), ro[:, 3:4], -1.0, ro[:, 2:3], MUL, ADD), [RO], [ck(8)])
+    op("v", ts(col(14), kf[:, 2:3], -1.0, None, MUL), [KF], [ck(14)])
+    op("v", tt(col(3), T.uu[:, 0:1], T.uu[:, 1:2], MUL), [("uu", 0, 2)], [ck(3)])
+    op("v", ts(col(5), ro[:, 3:4], -17.0, col(4), MUL, ADD), [RO, ck(4)], [ck(5)])
+    op("v", ts(col(7), ro[:, 3:4], -129.0, col(6), MUL, ADD), [RO, ck(6)], [ck(7)])
+    op("v", lambda e: e.memset(T.erw[:], 0.0), [], [("erw", 0, 144)])
+    op("v", tt(col(9), col(8), col(3), MUL), [ck(8), ck(3)], [ck(9)])
+    op("v", tt(col(10), col(5), col(3), MUL), [ck(5), ck(3)], [ck(10)])
+    op("v", tt(col(11), col(7), col(3), MUL), [ck(7), ck(3)], [ck(11)])
+    op("v", ts(col(12), kf[:, 2:3], 3.0, col(5), EQ, MUL), [KF, ck(5)], [ck(12)])
+    op("v", ts(T.erw[:, 15:128:16], T.gbd[:, 0:128:16], col(12), None, MUL), [GBD, ck(12)], [("erw", 0, 144)])
+    op("v", ts(T.fa[:], R(4), 0.0, 512.0, EQ, MUL), [RK(4)], [("fa", 0, W)])
+    op("v", ts(T.fra[:], R(1), 10.0, 512.0, EQ, MUL), [RK(1)], [("fra", 0, W)])
+    op("v", ts(T.frb[:], R(1), 11.0, None, EQ), [RK(1)], [("frb", 0, W)])
+    op("v", ts(T.frc[:], R(1), 9.0, 512.0, EQ, MUL), [RK(1)], [("frc", 0, W)])
+    op("v", ts(T.frd[:], R(1), 8.0, 262144.0, EQ, MUL), [RK(1)], [("frd", 0, W)])
+    op("v", ts(T.g11[:], T.gbd[:, 0:W], T.dm[:, 11:12], None, MUL), [GBD, DM], [("g11", 0, W)])
+    op("v", tt(T.idh[:], T.gbd[:, 0:W], T.dm[:], MUL), [GBD, DM], [("idh", 0, W)])
+    op("v", tt(T.fr2[:], T.fra[:], T.frb[:], ADD), [("fra", 0, W), ("frb", 0, W)], [("fr2", 0, W)])
+    op("v", tt(T.fr3[:], T.frc[:], T.frd[:], ADD), [("frc", 0, W), ("frd", 0, W)], [("fr3", 0, W)])
+    op("v", tt(T.r2a[:], T.idh[:], T.fa[:], MUL), [("idh", 0, W), ("fa", 0, W)], [("r2a", 0, W)])
+    op("v", tt(T.r2b[:], T.g11[:], T.fr2[:], MUL), [("g11", 0, W), ("fr2", 0, W)], [("r2b", 0, W)])
+    op("v", tt(T.fr4[:], T.fr2[:], T.fr3[:], ADD), [("fr2", 0, W), ("fr3", 0, W)], [("fr4", 0, W)])
+    op("v", tt(T.r2[:], T.r2a[:], T.r2b[:], ADD), [("r2a", 0, W), ("r2b", 0, W)], [("r2", 0, W)])
+    op("v", tt(T.r4[:], T.g11[:], T.fr4[:], MUL), [("g11", 0, W), ("fr4", 0, W)], [("r4", 0, W)])
+    for t in range(4):
+        op("v", ts(T.gw[:, 136 * t:136 * t + W], T.gbd[:, 96:224], col(10), None, MUL), [GBD, ck(10)], [("gw", 136 * t, 136 * t + W)])
+        op("v", ts(T.gw[:, 136 * t + W:136 * t + 136], T.gbd[:, 32 * t:32 * t + 128:16], col(9), None, MUL), [GBD, ck(9)], [("gw", 136 * t + W, 136 * t + 136)])
+    op("v", ts(T.gl[:, 0:128], T.gbd[:, 96:224], col(10), None, MUL), [GBD, ck(10)], [("gl", 0, 128)])
+    op("v", ts(T.gl[:, 128:256], T.gbd[:, 64:192], col(9), None, MUL), [GBD, ck(9)], [("gl", 128, 256)])
+    op("v", ts(T.gl[:, 256:384], T.gbd[:, 96:224], col(11), None, MUL), [GBD, ck(11)], [("gl", 256, 384)])
+    op("v", ts(T.gl[:, 384:512], T.gbd[:, 96:224], col(9), None, MUL), [GBD, ck(9)], [("gl", 384, 512)])
+    op("v", cp(T.gb8[:], T.gbd[:, 0:128:16]), [GBD], [("gb8", 0, 8)])
+    for r in range(16):
+        op("s", act(T.tab[:, r:2048:16], R(5), AF.Identity, bias=T.b16[:, r:r + 1], scale=ro[:, 0:1]),
+           [RK(5), ("b16", 0, 16), ("ro", 0, 1)], [("tab", 0, 2048)])
+    for r in range(16):
+        op("s", act(T.e16[:, W * r:W * r + W], T.gbd[:, 0:W], AF.Copy, scale=T.d16[:, r:r + 1]),
+           [("gbd", 0, W), ("d16", 0, 16)], [("e16", W * r, W * r + W)])
+
+    nxl = T.landA[:, 0:64, :]
+    dma("y", T.s2r[0:32, :], nxl, [("landAn", 0, 1)], [("s2h", 0, 512)], [arrA])
+    dma("y", T.s2r[32:64, :], nxl, [("landAn", 0, 1)], [("s2l", 0, 512)], [arrA])
+    dma("s", T.s2r[64:96, :], T.landA[:, 64:128, :], [("landAw", 0, 1)], [("s2w", 0, 512)], [arrA])
+    dma("s", T.l1r[:], nxl, [("landAn", 0, 1)], [("l1r", 0, W)], [arrA])
+    for t in range(4):
+        for r0, r1, sh in ((0, 4 - t, t), (4 - t, 4, t - 4)):
+            if r0 < r1:
+                dma("y", T.ep[32 * (r0 + sh):32 * (r1 + sh), :, 16 * t:16 * t + 16],
+                    T.landE[r0:r1, t // 2::2, 16 * (t % 2):16 * (t % 2) + 16], [("landE", 0, 1)], [("ep%d%d" % (t, r0), 0, 1)], [arrE])
+    dma("y", T.xr[:], T.landX[:], [("landX", 0, 1)], [("xr", 0, 16)], [arrX])
+    EPK = [("ep%d%d" % (t, r0), 0, 1) for t in range(4) for r0 in (0, 4 - t) if r0 < 4]
+
+    for h in range(2):
+        lo, hi = 256 * h, 256 * h + 256
+        op("v", ts(T.s2r[0:32, lo:hi], T.s2r[0:32, lo:hi], 127, None, AND), [("s2h", lo, hi)], [("s2h", lo, hi)])
+        op("v", cp(T.s2f[0:96, lo:hi], T.s2r[0:96, lo:hi]), [("s2h", lo, hi), ("s2l", lo, hi), ("s2w", lo, hi)], [("s2f", lo, hi)])
+        for v in range(4):
+            op("p", mm(T["pb%d" % v][:, lo:hi], T.lbv[:, W * v:W * v + W], T.s2f[:, lo:hi]),
+               [("lbv", W * v, W * v + W), ("s2f", lo, hi), ("s2k", lo, hi)], [("pb%d" % v, 0, 1)])
+    op("v", cp(T.l1[:], T.l1r[:]), [("l1r", 0, W)], [("l1", 0, W)])
+    for v in range(4):
+        lo, hi = 512 * v, 512 * v + 512
+        if v % 2 == 0:
+            op("s", act(T.t0[:, lo:hi], T["pb%d" % v][:]), [("pb%d" % v, 0, 1)], [("t0", lo, hi)])
+        else:
+            op("v", cp(T.t0[:, lo:hi], T["pb%d" % v][:]), [("pb%d" % v, 0, 1)], [("t0", lo, hi)])
+    for v in range(4):
+        op("p", mm(T["pb%d" % (4 + v)][:], T.liv[:, W * v:W * v + W], T.s2f[:]),
+           [("liv", W * v, W * v + W), ("s2f", 0, 512), ("s2k", 0, 512)], [("pb%d" % (4 + v), 0, 1)])
+
+    def gather(q, out, okey, lo, hi, win, wkey, w0, lst, lkey):
+        src = win[:, w0:w0 + 2048].indirect(lst[:, lo // 16:hi // 16])
+        rd = [(wkey, w0, w0 + 2048), (lkey, lo // 16, hi // 16)]
+        if q == "v":
+            op("v", cp(out[:, lo:hi], src), rd, [(okey, lo, hi)])
+        else:
+            op("s", act(out[:, lo:hi], src), rd, [(okey, lo, hi)])
+
+    def relay(h, pbn, gbuf, gkey):
+        for r in range(16):
+            op("p", mm(T[pbn][:, 0:64], T.erw[:, 15 - r:143 - r], gbuf[:, 1024 * h + r:1024 * h + 1024:16], r == 0, r == 15),
+               [("erw", 0, 144), (gkey, 1024 * h, 1024 * h + 1024)], [(pbn, 0, 1)])
+
+    def relist(h, pbn, lst, lkey):
+        op("v", cp(lst[:, 64 * h:64 * h + 64], T[pbn][:, 0:64]), [(pbn, 0, 1)], [(lkey, 64 * h, 64 * h + 64)])
+
+    SPL = [("v", 0, 384), ("s", 384, 1024), ("v", 1024, 1408), ("s", 1408, 2048)]
+    for q, lo, hi in SPL:
+        gather(q, T.ga, "ga", lo, hi, T.t0, "t0", 0, T.l1, "l1")
+    relay(0, "pb0", T.ga, "ga")
+    relay(1, "pb1", T.ga, "ga")
+    for h in range(2):
+        for r in range(16):
+            b = "pb%d" % (4 + r // 4)
+            s = slice(1024 * h + r, 1024 * h + 1024, 16)
+            op("v", tt(T.t1[:, s], T.ga[:, s], T[b][:, (r % 4) * 128 + 64 * h:(r % 4) * 128 + 64 * h + 64], MAX),
+               [("ga", 1024 * h, 1024 * h + 1024), (b, 0, 1)], [("t1", 1024 * h, 1024 * h + 1024)])
+        relist(h, "pb%d" % h, T.l2, "l2")
+    I2 = ["pb2", "pb3", "pb4", "pb5"]
+
+    def in2(c):
+        op("p", mm(T[I2[c]][:], T.r2[:], T.t1[:, 512 * c:512 * c + 512]), [("r2", 0, W), ("t1", 512 * c, 512 * c + 512)], [(I2[c], 0, 1)])
+
+    def fix2(c):
+        lo, hi = 512 * c, 512 * c + 512
+        op("v", tt(T.tab[:, 2048 + lo:2048 + hi], T.gb[:, lo:hi], T[I2[c]][:], MAX), [("gb", lo, hi), (I2[c], 0, 1)], [("tab", 2048 + lo, 2048 + hi)])
+    for q, lo, hi in SPL:
+        gather(q, T.gb, "gb", lo, hi, T.t1, "t1", 0, T.l2, "l2")
+    in2(0)
+    in2(1)
+    in2(2)
+    relay(0, "pb0", T.gb, "gb")
+    in2(3)
+    relay(1, "pb1", T.gb, "gb")
+    fix2(0)
+    fix2(1)
+    for l in range(2):
+        op("v", ts(T.ei[:, 64 * l:64 * l + 64], T.ep[:, l, :], 3, None, ADD), EPK, [("ei", 64 * l, 64 * l + 64)])
+    op("v", ts(T.xa[:], T.xr[:], 127, None, AND), [("xr", 0, 16)], [("xa", 0, 16)])
+    op("v", ts(T.xb[:], T.xr[:], 7, None, SHR), [("xr", 0, 16)], [("xb", 0, 16)])
+    op("v", ts(T.fi[:], T.ei[:], 3, None, AND), [("ei", 0, W)], [("fi", 0, W)])
+    op("v", ts(T.ki[:], T.ei[:], 2, None, SHR), [("ei", 0, W)], [("ki", 0, W)])
+    fix2(2)
+    op("v", ts(T.xc[:], T.xa[:], 16, None, MUL), [("xa", 0, 16)], [("xc", 0, 16)])
+    op("v", cp(T.fb[:], T.fi[:]), [("fi", 0, W)], [("fb", 0, W)])
+    op("v", ts(T.off[:], T.ki[:], 2048, None, MUL), [("ki", 0, W)], [("off", 0, W)])
+    relist(0, "pb0", T.l4, "l4")
+    op("v", tt(T.xd[:], T.xc[:], T.xb[:], ADD), [("xc", 0, 16), ("xb", 0, 16)], [("xd", 0, 16)])
+    fix2(3)
+    relist(1, "pb1", T.l4, "l4")
+    C4 = ["pb6", "pb7", "pb2", "pb3"]
+    for c in range(4):
+        op("p", mm(T[C4[c]][:], T.r4[:], T.tab[:, 2048 + 512 * c:2560 + 512 * c]), [("r4", 0, W), ("tab", 2048 + 512 * c, 2560 + 512 * c)], [(C4[c], 0, 1)])
+    EMB = ["pb0", "pb1", "pb4", "pb5"]
+
+    def em_rows(c):
+        for r in range(16):
+            op("p", mm(T[EMB[c]][:, r:512:16], T.e16[:, W * r:W * r + W], T.fb[:, 32 * c:32 * c + 32]),
+               [("e16", W * r, W * r + W), ("fb", 32 * c, 32 * c + 32)], [(EMB[c], 0, 1)])
+
+    def em_sq(c):
+        op("s", act(T.sq[:, 512 * c:512 * c + 512], T[EMB[c]][:], AF.Square, bias=col(14)), [(EMB[c], 0, 1), ck(14)], [("sq", 512 * c, 512 * c + 512)])
+
+    def em_mask(c):
+        op("s", act(T.em[:, 512 * c:512 * c + 512], T.sq[:, 512 * c:512 * c + 512], AF.Relu, bias=1.0, scale=-1.0), [("sq", 512 * c, 512 * c + 512)], [("em", 512 * c, 512 * c + 512)])
+    for c in range(4):
+        em_rows(c)
+
+    def fixb(k, gbuf, gkey, lo, hi):
+        c = lo // 512
+        o = 2048 * k + 2048
+        op("v", tt(T.tab[:, o + lo:o + hi], gbuf[:, lo:hi], T[C4[c]][:, lo - 512 * c:hi - 512 * c], MAX),
+           [(gkey, lo, hi), (C4[c], 0, 1)], [("tab", o + lo, o + hi)])
+    gather("v", T.ga, "ga", 0, 640, T.tab, "tab", 2048, T.l4, "l4")
+    for lo, hi in ((640, 1024), (1024, 1536), (1536, 2048)):
+        gather("s", T.ga, "ga", lo, hi, T.tab, "tab", 2048, T.l4, "l4")
+    for c in range(4):
+        fixb(1, T.ga, "ga", 512 * c, 512 * c + 512)
+    op("s", act(T.c4a[:, 0:512], T[C4[0]][:]), [(C4[0], 0, 1)], [("c4a", 0, 512)])
+    op("s", act(T.c4a[:, 512:640], T[C4[1]][:, 0:128]), [(C4[1], 0, 1)], [("c4a", 512, 640)])
+    op("v", tt(T.xe[:], T.xd[:], T.off[:, 0:16], ADD), [("xd", 0, 16), ("off", 0, 16)], [("xe", 0, 16)])
+    for k in (2, 3):
+        gbuf, gkey = (T.gb, "gb") if k == 2 else (T.ga, "ga")
+        o = 2048 * k + 2048
+        op("v", tt(T.tab[:, o:o + 640], T.tab[:, o - 2048:o].indirect(T.l4[:, 0:40]), T.c4a[:], MAX),
+           [("tab", o - 2048, o), ("l4", 0, 40), ("c4a", 0, 640)], [("tab", o, o + 640)])
+        for lo, hi in ((1024, 1536), (1536, 2048), (640, 1024)):
+            gather("s", gbuf, gkey, lo, hi, T.tab, "tab", o - 2048, T.l4, "l4")
+        for lo, hi in ((1024, 1536), (1536, 2048), (640, 1024)):
+            fixb(k, gbuf, gkey, lo, hi)
+        if k == 2:
+            em_sq(0)
+        else:
+            em_mask(0)
+            for c in (1, 2, 3):
+                em_sq(c)
+                em_mask(c)
+    for b in range(2):
+        op("v", cp(T["ql%d" % b][:], T.xe[:, 8 * b:8 * b + 8]), [("xe", 0, 16)], [("ql%d" % b, 0, 8)])
+
+    PX, PL = ["pb6", "pb7"], ["pb2", "pb3"]
+
+    def step(t, b):
+        q, x = "ql%d" % b, "x%d" % b
+        lo = 256 * t + 128 * b
+        op("v", tt(T[x][:], T.tab[:].indirect(T[q][:]), T.em[:, lo:lo + 128], MUL), [("tab", 0, 10240), (q, 0, 8), ("em", lo, lo + 128)], [(x, 0, W)])
+        if t < 6:
+            c = 136 * (t % 4)
+            op("p", mm(T[PX[b]][:, 0:136], T[x][:], T.gw[:, c:c + 136]), [(x, 0, W), ("gw", c, c + 136)], [(PX[b], 0, 1)])
+        else:
+            c = 256 * (t - 6)
+            op("p", mm(T[PX[b]][:, 0:256], T[x][:], T.gl[:, c:c + 256]), [(x, 0, W), ("gl", c, c + 256)], [(PX[b], 0, 1)])
+        if t < 7:
+            o = 16 * (t + 1) + 8 * b
+            op("p", mm(T[PL[b]][:, 0:8], T.idh[:], T.off[:, o:o + 8], True, False), [("idh", 0, W), ("off", o, o + 8)], [(PL[b], 0, 1)])
+
+    def turn(t, b):
+        y = "y%d" % b
+        op("v", tt(T[y][:], T[PX[b]][:, 0:128], T.dm[:], MUL), [(PX[b], 0, 1), DM], [(y, 0, W)])
+        op("p", mm(T[PL[b]][:, 0:8], T[y][:], T.gb8[:], t == 7, True), [(y, 0, W), ("gb8", 0, 8)], [(PL[b], 0, 1)])
+
+    def weigh(t, b):
+        a = T.acc[:, 8 * b:8 * b + 8]
+        if t == 0:
+            op("v", cp(a, T[PX[b]][:, 128:136]), [(PX[b], 0, 1)], [("acc", 8 * b, 8 * b + 8)])
+        elif t < 6:
+            op("v", tt(a, a, T[PX[b]][:, 128:136], MAX), [(PX[b], 0, 1), ("acc", 8 * b, 8 * b + 8)], [("acc", 8 * b, 8 * b + 8)])
+        else:
+            yw = "yw%d" % b
+            op("v", tt(T[yw][:], T[PX[b]][:, 128:256], T.dm[:], MUL), [(PX[b], 0, 1), DM], [(yw, 0, W)])
+            pw = ("pb0", "pb1")[b]
+            op("p", mm(T[pw][:, 0:8], T[yw][:], T.gbd[:, 0:128:16]), [(yw, 0, W), ("gbd", 0, W)], [(pw, 0, 1)])
+
+    def relq(b):
+        q = "ql%d" % b
+        op("v", cp(T[q][:], T[PL[b]][:, 0:8]), [(PL[b], 0, 1)], [(q, 0, 8)])
+
+    step(0, 0)
+    step(0, 1)
+    for t in range(7):
+        turn(t, 0)
+        turn(t, 1)
+        weigh(t, 0)
+        relq(0)
+        step(t + 1, 0)
+        weigh(t, 1)
+        relq(1)
+        step(t + 1, 1)
+        if t == 5:
+            for r in range(16):
+                op("s", act(T.yp[:, r:256:16], T.acc[:], AF.Copy, scale=T.d16[:, r:r + 1]), [("acc", 0, 16), ("d16", 0, 16)], [("yp", 0, 256)])
+    for b in range(2):
+        pw = ("pb4", "pb5")[b]
+        op("p", mm(T[pw][:, 0:8], T.yp[:, W * b:W * b + W], T.gbd[:, 0:128:16]), [("yp", 0, 256), ("gbd", 0, W)], [(pw, 0, 1)])
+    for b in range(2):
+        s = slice(8 * b, 8 * b + 8)
+        op("v", cp(T.m06[:, s], T[("pb0", "pb1")[b]][:, 0:8]), [(("pb0", "pb1")[b], 0, 1)], [("m06", 8 * b, 8 * b + 8)])
+    turn(7, 0)
+    weigh(7, 0)
+    turn(7, 1)
+    weigh(7, 1)
+    for b in range(2):
+        s = slice(8 * b, 8 * b + 8)
+        op("v", tt(T.m05[:, s], T.m06[:, s], T[("pb4", "pb5")[b]][:, 0:8], MAX), [("m06", 8 * b, 8 * b + 8), (("pb4", "pb5")[b], 0, 1)], [("m05", 8 * b, 8 * b + 8)])
+    for b in range(2):
+        op("v", cp(T.outb[:, 8 * b:8 * b + 8], T[PL[b]][:, 0:8]), [(PL[b], 0, 1)], [("outb", 8 * b, 8 * b + 8)])
+        s = slice(8 * b, 8 * b + 8)
+        pw = ("pb0", "pb1")[b]
+        op("v", tt(T.outb[:, 16 + 8 * b:24 + 8 * b], T.m05[:, s], T[pw][:, 0:8], MAX), [("m05", 8 * b, 8 * b + 8), (pw, 0, 1)], [("outb", 16 + 8 * b, 24 + 8 * b)])
+
+    arrO = send(lambda s: T.outb[:], T.landO[rank], "arrO", "locO", [("outb", 0, 32)])
+    dma("y", T.landO[rank], T.outb[:], [("outb", 0, 32)], [("landO", 0, 1)])
+    dma("y", T.last[:], T.landO[:, rows, 0:16], [("landO", 0, 1)], [], [arrO])
+    dma("s", T.peak[:], T.landO[:, rows, 16:32], [("landO", 0, 1)], [], [arrO])
+    for sem, val in total.items():
+        if known["g"].get(sem, 0) < val:
+            g.wait_ge(T.sem[sem], val)

@@ -7,34 +7,27 @@ SCRATCH = {
     "srcA": ("dram", [4, 128, 64], "int32"), "srcE": ("dram", [4, 128, 32], "int32"), "srcX": ("dram", [4, 128, 4], "int32"),
     "landA": ("dram", [4, 128, 64], "int32"), "landE": ("dram", [4, 128, 32], "int32"), "landX": ("dram", [4, 128, 4], "int32"),
     "landO": ("dram", [4, 128, 32], "float32"),
-    "s2r": ("sbuf", [128, 512], "int32"), "s2f": ("sbuf", [128, 512], "float16"), "l1r": ("sbuf", [128, 128], "int32"),
+    "s2r": ("sbuf", [128, 512], "int32"), "s2f": ("sbuf", [128, 512], "float16"), "l1r": ("sbuf", [128, 128], "int32"), "l1f": ("sbuf", [128, 128], "float16"),
     "ep": ("sbuf", [128, 2, 64], "int32"), "ei": ("sbuf", [128, 128], "int32"), "fi": ("sbuf", [128, 128], "int32"), "ki": ("sbuf", [128, 128], "int32"),
-    "fb": ("sbuf", [128, 128], "bfloat16"), "off": ("sbuf", [128, 128], "float16"),
-    "xr": ("sbuf", [128, 16], "int32"), "xa": ("sbuf", [128, 16], "int32"), "xb": ("sbuf", [128, 16], "int32"), "xc": ("sbuf", [128, 16], "int32"), "xd": ("sbuf", [128, 16], "int32"), "xe": ("sbuf", [128, 16], "int32"),
+    "fb": ("sbuf", [128, 128], "bfloat16"), "off": ("sbuf", [128, 128], "float16"), "xr": ("sbuf", [128, 16], "int32"), "xe": ("sbuf", [128, 16], "int32"),
     "t0": ("sbuf", [128, 2048], "bfloat16"), "t1": ("sbuf", [128, 2048], "bfloat16"), "tab": ("sbuf", [128, 10240], "bfloat16"),
     "ga": ("sbuf", [128, 2048], "bfloat16"), "gb": ("sbuf", [128, 2048], "bfloat16"), "c4a": ("sbuf", [128, 640], "bfloat16"),
     "l1": ("sbuf", [128, 128], "uint16"), "l2": ("sbuf", [128, 128], "uint16"), "l4": ("sbuf", [128, 128], "uint16"),
-    "sq": ("sbuf", [128, 2048], "bfloat16"), "em": ("sbuf", [128, 2048], "bfloat16"),
+    "ec": ("sbuf", [128, 2048], "bfloat16"), "em": ("sbuf", [128, 2048], "bfloat16"),
     "ql0": ("sbuf", [128, 8], "uint16"), "ql1": ("sbuf", [128, 8], "uint16"),
     "x0": ("sbuf", [128, 128], "bfloat16"), "x1": ("sbuf", [128, 128], "bfloat16"),
-    "y0": ("sbuf", [128, 128], "float16"), "y1": ("sbuf", [128, 128], "float16"),
-    "acc": ("sbuf", [128, 16], "float32"), "yp": ("sbuf", [128, 256], "bfloat16"),
-    "yw0": ("sbuf", [128, 128], "bfloat16"), "yw1": ("sbuf", [128, 128], "bfloat16"),
-    "m05": ("sbuf", [128, 16], "float32"), "m06": ("sbuf", [128, 16], "float32"), "outb": ("sbuf", [128, 32], "float32"),
-    "mi": ("sbuf", [128, 128], "int32"), "kq": ("sbuf", [128, 8], "int32"), "kc": ("sbuf", [128, 8], "int32"), "kf": ("sbuf", [128, 8], "float32"),
-    "ri": ("sbuf", [128, 6, 128], "int32"), "rf": ("sbuf", [128, 7, 128], "bfloat16"),
-    "ro": ("sbuf", [128, 4], "float32"), "rb": ("sbuf", [128, 4], "float32"), "mv": ("sbuf", [128, 4], "float32"),
-    "uu": ("sbuf", [128, 2], "float32"), "cf": ("sbuf", [128, 24], "float32"),
-    "gbd": ("sbuf", [128, 256], "bfloat16"), "dm": ("sbuf", [128, 128], "bfloat16"), "d16": ("sbuf", [128, 16], "float32"),
-    "e16": ("sbuf", [128, 2048], "bfloat16"), "b16": ("sbuf", [128, 16], "float32"),
-    "erw": ("sbuf", [128, 144], "bfloat16"), "gw": ("sbuf", [128, 544], "bfloat16"), "gl": ("sbuf", [128, 512], "bfloat16"),
-    "gb8": ("sbuf", [128, 8], "float16"), "idh": ("sbuf", [128, 128], "float16"),
-    "ka": ("sbuf", [128, 128], "bfloat16"), "kb": ("sbuf", [128, 128], "bfloat16"), "kd": ("sbuf", [128, 128], "bfloat16"), "ke": ("sbuf", [128, 128], "bfloat16"),
-    "lb": ("sbuf", [128, 128], "bfloat16"), "li": ("sbuf", [128, 128], "bfloat16"), "lbv": ("sbuf", [128, 512], "float16"), "liv": ("sbuf", [128, 512], "float16"),
-    "f1": ("sbuf", [128, 128], "bfloat16"), "f2": ("sbuf", [128, 128], "bfloat16"), "f3": ("sbuf", [128, 128], "bfloat16"),
-    "fa": ("sbuf", [128, 128], "bfloat16"), "fra": ("sbuf", [128, 128], "bfloat16"), "frb": ("sbuf", [128, 128], "bfloat16"), "frc": ("sbuf", [128, 128], "bfloat16"), "frd": ("sbuf", [128, 128], "bfloat16"),
-    "fr2": ("sbuf", [128, 128], "bfloat16"), "fr3": ("sbuf", [128, 128], "bfloat16"), "fr4": ("sbuf", [128, 128], "bfloat16"),
-    "g11": ("sbuf", [128, 128], "bfloat16"), "r2a": ("sbuf", [128, 128], "bfloat16"), "r2b": ("sbuf", [128, 128], "bfloat16"), "r2": ("sbuf", [128, 128], "bfloat16"), "r4": ("sbuf", [128, 128], "bfloat16"),
+    "y0": ("sbuf", [128, 128], "float16"), "y1": ("sbuf", [128, 128], "float16"), "yw0": ("sbuf", [128, 256], "float16"), "yw1": ("sbuf", [128, 256], "float16"),
+    "acc": ("sbuf", [128, 16], "float32"), "outb": ("sbuf", [128, 32], "float32"),
+    "kq": ("sbuf", [128, 9], "int32"), "kc": ("sbuf", [128, 9], "int32"), "kf": ("sbuf", [128, 9], "float32"),
+    "rm": ("sbuf", [128, 128], "bfloat16"), "rc": ("sbuf", [128, 128], "bfloat16"), "rg": ("sbuf", [128, 256], "bfloat16"), "rs": ("sbuf", [128, 128], "bfloat16"),
+    "one": ("sbuf", [128, 128], "bfloat16"), "sel": ("sbuf", [128, 128], "bfloat16"), "keep": ("sbuf", [128, 128], "bfloat16"),
+    "ro": ("sbuf", [128, 3], "float32"), "rb": ("sbuf", [128, 3], "float32"), "mv": ("sbuf", [128, 4], "float32"), "cf": ("sbuf", [128, 24], "float32"),
+    "gbd": ("sbuf", [128, 256], "bfloat16"), "d16": ("sbuf", [128, 16], "float32"), "b16": ("sbuf", [128, 16], "float32"),
+    "e16": ("sbuf", [128, 2048], "bfloat16"), "erw": ("sbuf", [128, 144], "bfloat16"), "pc": ("sbuf", [128, 16], "bfloat16"), "wc": ("sbuf", [128, 16], "bfloat16"),
+    "idh": ("sbuf", [128, 128], "float16"),
+    "la": ("sbuf", [128, 128], "bfloat16"), "lc": ("sbuf", [128, 128], "bfloat16"), "lb": ("sbuf", [128, 128], "bfloat16"), "li": ("sbuf", [128, 128], "bfloat16"),
+    "lbv": ("sbuf", [128, 512], "float16"), "liv": ("sbuf", [128, 512], "float16"),
+    "r2a": ("sbuf", [128, 128], "bfloat16"), "r2b": ("sbuf", [128, 128], "bfloat16"), "r2": ("sbuf", [128, 128], "bfloat16"), "r4": ("sbuf", [128, 128], "bfloat16"),
 }
 for _i in range(8):
     SCRATCH["pb%d" % _i] = ("psum", [128, 512], "float32")
@@ -151,6 +144,13 @@ def rank_program(g, core, T, topo):
     def mm(out, lhsT, rhs, start=True, stop=True):
         return lambda e: e.matmul(out, lhsT, rhs, start, stop)
 
+    def iota(out, pattern, base=0):
+        return lambda e: e.iota(out, pattern, base, 0, allow_small_or_imprecise_dtypes=True)
+
+    def asel(out, in_, pattern, cmp_, fill, base):
+        return lambda e: e.affine_select(out, in_, pattern, cmp_, fill, base, 0)
+    W = 128
+
     A3, E3, X3 = T.srcA, T.srcE, T.srcX
     dma("y", A3[:, 0:64, :], T.nx[:], [], [("srcAn", 0, 1)])
     dma("s", A3[:, 64:128, :], T.w[:], [], [("srcAw", 0, 1)])
@@ -163,119 +163,94 @@ def rank_program(g, core, T, topo):
     dma("y", T.landE[rank], T.e[rows, :], [], [("landE", 0, 1)])
     dma("s", T.landX[rank], T.x[rows, :], [], [("landX", 0, 1)])
 
-    op("g", lambda e: e.iota(T.kq[:], [[0, 8]], 0, 1), [], [("kq", 0, 8)])
-    op("g", lambda e: e.iota(T.mi[:], [[1, 128]], 0, 0), [], [("mi", 0, 128)])
+    op("g", lambda e: e.iota(T.kq[:], [[0, 9]], 0, 1), [], [("kq", 0, 9)])
+    op("g", iota(T.rm[:], [[1, 128]]), [], [("rm", 0, W)])
+    op("g", iota(T.rg[:], [[0, 2], [1, 8], [0, 16]]), [], [("rg", 0, 256)])
+    op("g", iota(T.rc[:], [[1, 32], [0, 4]]), [], [("rc", 0, W)])
     arrA = send(lambda s: A3[s], T.landA[rank], "arrA", "locA", [("srcAn", 0, 1), ("srcAw", 0, 1)])
+    op("g", asel(T.rs[:], T.rc[:], [[0, 32], [1, 4]], AluOpType.is_gt, -1.0, 0), [("rc", 0, W)], [("rs", 0, W)])
+    op("g", iota(T.one[:], [[0, 128]], 1), [], [("one", 0, W)])
+    op("g", asel(T.sel[:], T.one[:], [[0, 32], [-1, 4]], AluOpType.is_gt, 0.0, 2), [("one", 0, W)], [("sel", 0, W)])
+    op("g", asel(T.keep[:], T.sel[:], [[0, 8], [1, 4], [0, 4]], AluOpType.not_equal, 1.0, -2), [("sel", 0, W)], [("keep", 0, W)])
     arrE = send(lambda s: E3[s], T.landE[rank], "arrE", "locE", [("srcE", 0, 1)])
     arrX = send(lambda s: X3[s], T.landX[rank], "arrX", "locX", [("srcX", 0, 1)])
 
     kf, ro, rb, mv, cf = T.kf, T.ro, T.rb, T.mv, T.cf
-    KQ, KC = T.kq, T.kc
     for i, (o1, a1, o2, a2) in enumerate([(SHR, 4, None, 0), (AND, 15, None, 0), (AND, 3, None, 0), (SHR, 2, AND, 3),
-                                          (SHR, 5, None, 0), (SHR, 2, AND, 7), (AND, 1, None, 0), (SHR, 1, AND, 1)]):
-        c = ts(KC[:, i:i + 1], KQ[:, i:i + 1], a1, None, o1) if o2 is None else ts(KC[:, i:i + 1], KQ[:, i:i + 1], a1, a2, o1, o2)
-        op("v", c, [("kq", 0, 8)], [("kc", i, i + 1)])
-    op("v", cp(kf[:], KC[:]), [("kc", 0, 8)], [("kf", 0, 8)])
-    for i, (o1, a1, o2, a2) in enumerate([(SHR, 4, None, 0), (AND, 15, None, 0), (SHR, 2, AND, 3), (AND, 1, None, 0), (SHR, 1, AND, 1)]):
-        c = ts(T.ri[:, i, :], T.mi[:], a1, None, o1) if o2 is None else ts(T.ri[:, i, :], T.mi[:], a1, a2, o1, o2)
-        op("v", c, [("mi", 0, 128)], [("ri%d" % i, 0, 128)])
-    op("v", cp(T.rf[:, 5, :], T.mi[:]), [("mi", 0, 128)], [("rf5", 0, 128)])
-    for i in range(5):
-        op("v", cp(T.rf[:, i, :], T.ri[:, i, :]), [("ri%d" % i, 0, 128)], [("rf%d" % i, 0, 128)])
+                                          (SHR, 5, None, 0), (SHR, 2, AND, 7), (AND, 1, None, 0), (SHR, 1, AND, 1), (AND, 127, None, 0)]):
+        c = ts(T.kc[:, i:i + 1], T.kq[:, i:i + 1], a1, None, o1) if o2 is None else ts(T.kc[:, i:i + 1], T.kq[:, i:i + 1], a1, a2, o1, o2)
+        op("v", c, [("kq", 0, 9)], [("kc", i, i + 1)])
+    op("v", cp(kf[:], T.kc[:]), [("kc", 0, 9)], [("kf", 0, 9)])
+    KF, RM, RC = ("kf", 0, 9), ("rm", 0, W), ("rc", 0, W)
 
-    def R(i):
-        return T.rf[:, i, :]
-
-    def RK(i):
-        return ("rf%d" % i, 0, 128)
-    KF = ("kf", 0, 8)
+    def k(i):
+        return kf[:, i:i + 1]
 
     def col(i):
         return cf[:, i:i + 1]
 
     def ck(i):
         return ("cf", i, i + 1)
-    W = 128
-    for h in range(2):
-        op("v", ts(T.gbd[:, W * h:W * h + W], R(0), kf[:, 0:1], None, EQ), [RK(0), KF], [("gbd", W * h, W * h + W)])
-    op("v", ts(T.dm[:], R(1), kf[:, 1:2], None, EQ), [RK(1), KF], [("dm", 0, W)])
+
+    def cts(i, in0, s1, s2, ops, reads):
+        op("v", ts(col(i), in0, s1, s2, *ops), reads, [ck(i)])
+    for j in range(3):
+        op("v", ts(ro[:, j:j + 1], k(3), float(j), None, EQ), [KF], [("ro", j, j + 1)])
+    op("v", ts(T.d16[:], T.rm[:, 0:16], k(1), None, EQ), [RM, KF], [("d16", 0, 16)])
+    op("v", ts(T.b16[:], T.rm[:, 0:16], ro[:, 1:2], None, MUL), [RM, ("ro", 1, 2)], [("b16", 0, 16)])
+    op("v", ts(T.gbd[:], T.rg[:], k(0), None, EQ), [("rg", 0, 256), KF], [("gbd", 0, 256)])
+    for j in range(3):
+        op("v", ts(rb[:, j:j + 1], k(4), float(j), None, EQ), [KF], [("rb", j, j + 1)])
     for j in range(4):
-        op("v", ts(ro[:, j:j + 1], kf[:, 3:4], float(j), None, EQ), [KF], [("ro", j, j + 1)])
-        op("v", ts(rb[:, j:j + 1], kf[:, 4:5], float(j), None, EQ), [KF], [("rb", j, j + 1)])
-        op("v", ts(mv[:, j:j + 1], kf[:, 2:3], float(j), None, EQ), [KF], [("mv", j, j + 1)])
-    op("v", cp(T.d16[:], T.dm[:, 0:16]), [("dm", 0, 16)], [("d16", 0, 16)])
-    op("v", ts(T.b16[:], T.rf[:, 5, 0:16], ro[:, 1:2], 1.0, MUL, ADD), [RK(5), ("ro", 1, 2)], [("b16", 0, 16)])
-    GBD, DM = ("gbd", 0, 256), ("dm", 0, W)
-    RO, RB = ("ro", 0, 4), ("rb", 0, 4)
-    op("v", ts(col(0), rb[:, 1:2], 0.0078125, rb[:, 0:1], MUL, ADD), [RB], [ck(0)])
-    op("v", ts(col(2), rb[:, 0:1], -0.0078125, None, MUL), [RB], [ck(2)])
-    op("v", ts(T.kd[:], R(0), kf[:, 5:6], None, EQ), [RK(0), KF], [("kd", 0, W)])
-    op("v", ts(T.f1[:], R(3), 0.0, 512.0, EQ, MUL), [RK(3)], [("f1", 0, W)])
-    op("v", ts(col(1), rb[:, 2:3], 1.0, col(0), MUL, ADD), [RB, ck(0)], [ck(1)])
-    op("v", ts(T.kb[:], R(2), 1.0, col(2), EQ, MUL), [RK(2), ck(2)], [("kb", 0, W)])
-    op("v", ts(T.f2[:], R(2), 2.0, None, EQ), [RK(2)], [("f2", 0, W)])
-    op("v", ts(T.ka[:], R(2), kf[:, 4:5], col(1), EQ, MUL), [RK(2), KF, ck(1)], [("ka", 0, W)])
-    op("v", tt(T.f3[:], T.f2[:], R(3), MUL), [("f2", 0, W), RK(3)], [("f3", 0, W)])
-    op("v", ts(T.ke[:], T.kb[:], rb[:, 3:4], None, ADD), [("kb", 0, W), RB], [("ke", 0, W)])
-    op("v", tt(T.ka[:], T.ka[:], T.ke[:], ADD), [("ka", 0, W), ("ke", 0, W)], [("ka", 0, W)])
-    op("v", tt(T.f1[:], T.f1[:], T.f3[:], ADD), [("f1", 0, W), ("f3", 0, W)], [("f1", 0, W)])
-    op("v", tt(T.lb[:], T.ka[:], T.kd[:], MUL), [("ka", 0, W), ("kd", 0, W)], [("lb", 0, W)])
-    op("v", tt(T.li[:], T.lb[:], T.f1[:], MUL), [("lb", 0, W), ("f1", 0, W)], [("li", 0, W)])
+        op("v", ts(mv[:, j:j + 1], k(2), float(j), None, EQ), [KF], [("mv", j, j + 1)])
+    cts(0, rb[:, 1:2], 0.0078125, rb[:, 0:1], (MUL, ADD), [("rb", 0, 2)])
+    cts(1, k(5), 4.0, k(4), (MUL, ADD), [KF])
+    cts(2, k(5), 4.0, 1.0, (MUL, ADD), [KF])
+    cts(3, rb[:, 0:1], -0.0078125, None, (MUL,), [("rb", 0, 1)])
+    cts(4, rb[:, 2:3], 1.0, col(0), (MUL, ADD), [("rb", 2, 3), ck(0)])
+    cts(5, ro[:, 1:2], 128.0, ro[:, 0:1], (MUL, ADD), [("ro", 0, 2)])
+    op("v", ts(T.lc[:], T.rc[:], col(2), col(3), EQ, MUL), [RC, ck(2), ck(3)], [("lc", 0, W)])
+    op("v", ts(T.la[:], T.rc[:], col(1), col(4), EQ, MUL), [RC, ck(1), ck(4)], [("la", 0, W)])
+    cts(6, k(2), 3.0, col(5), (EQ, MUL), [KF, ck(5)])
+    op("v", lambda e: e.memset(T.erw[:], 0.0), [], [("erw", 0, 144)])
+    op("v", tt(T.lb[:], T.la[:], T.lc[:], ADD), [("la", 0, W), ("lc", 0, W)], [("lb", 0, W)])
+    op("v", ts(T.idh[:], T.rm[:], k(8), None, EQ), [RM, KF], [("idh", 0, W)])
     for v in range(4):
         op("v", ts(T.lbv[:, W * v:W * v + W], T.lb[:], mv[:, v:v + 1], None, MUL), [("lb", 0, W), ("mv", v, v + 1)], [("lbv", W * v, W * v + W)])
-    op("v", ts(T.s2f[96:128, 0:128], T.rf[96:128, 5, :], 0.0, 1.0, MUL, ADD), [RK(5)], [("s2k", 0, 128)])
-    for z in range(1, 4):
-        op("v", ts(T.s2f[96:128, W * z:W * z + W], T.rf[96:128, 5, :], 0.0, 1.0, MUL, ADD), [RK(5)], [("s2k", W * z, W * z + W)])
+    op("v", ts(T.erw[:, 15:128:16], T.gbd[:, 0:128:16], col(6), None, MUL), [("gbd", 0, 256), ck(6)], [("erw", 0, 144)])
+    op("v", ts(T.pc[:], T.gbd[:, 0:256:16], col(5), None, MUL), [("gbd", 0, 256), ck(5)], [("pc", 0, 16)])
+    op("v", ts(T.wc[:], T.gbd[:, 0:256:16], ro[:, 2:3], None, MUL), [("gbd", 0, 256), ("ro", 2, 3)], [("wc", 0, 16)])
+    cts(7, k(6), 2.0, k(7), (MUL, ADD), [KF])
+    cts(8, k(0), 4.0, 7.0, (MUL, ADD), [KF])
+    cts(9, k(1), 10.0, None, (EQ,), [KF])
+    cts(10, k(1), 11.0, None, (EQ,), [KF])
+    cts(11, k(6), -1.0, 1.0, (MUL, ADD), [KF])
+    cts(12, k(8), 1.0, None, (ADD,), [KF])
+    cts(13, col(8), col(9), -5.0, (MUL, ADD), [ck(8), ck(9)])
+    cts(14, col(8), col(10), -5.0, (MUL, ADD), [ck(8), ck(10)])
+    cts(15, col(9), -1.0, col(11), (MUL, ADD), [ck(9), ck(11)])
+    cts(16, col(12), col(15), -1.0, (MUL, ADD), [ck(12), ck(15)])
+    op("v", ts(T.r4[:], T.rc[:], col(14), None, EQ), [RC, ck(14)], [("r4", 0, W)])
+    op("v", ts(T.r2a[:], T.rm[:], col(16), None, EQ), [RM, ck(16)], [("r2a", 0, W)])
+    op("v", ts(T.r2b[:], T.rs[:], col(13), None, EQ), [("rs", 0, W), ck(13)], [("r2b", 0, W)])
+    op("v", tt(T.r2[:], T.r2a[:], T.r2b[:], ADD), [("r2a", 0, W), ("r2b", 0, W)], [("r2", 0, W)])
+    op("v", tt(T.li[:], T.lb[:], T.keep[:], MUL), [("lb", 0, W), ("keep", 0, W)], [("li", 0, W)])
     for v in range(4):
         op("v", ts(T.liv[:, W * v:W * v + W], T.li[:], mv[:, v:v + 1], None, MUL), [("li", 0, W), ("mv", v, v + 1)], [("liv", W * v, W * v + W)])
-    op("v", ts(T.uu[:], kf[:, 6:8], 1.0 - 0.001953125, 0.001953125, MUL, ADD), [KF], [("uu", 0, 2)])
-    op("v", ts(col(4), ro[:, 0:1], 16.0, ro[:, 1:2], MUL, ADD), [RO], [ck(4)])
-    op("v", ts(col(6), ro[:, 1:2], 128.0, ro[:, 0:1], MUL, ADD), [RO], [ck(6)])
-    op("v", ts(col(8), ro[:, 3:4], -1.0, ro[:, 2:3], MUL, ADD), [RO], [ck(8)])
-    op("v", ts(col(14), kf[:, 2:3], -1.0, None, MUL), [KF], [ck(14)])
-    op("v", tt(col(3), T.uu[:, 0:1], T.uu[:, 1:2], MUL), [("uu", 0, 2)], [ck(3)])
-    op("v", ts(col(5), ro[:, 3:4], -17.0, col(4), MUL, ADD), [RO, ck(4)], [ck(5)])
-    op("v", ts(col(7), ro[:, 3:4], -129.0, col(6), MUL, ADD), [RO, ck(6)], [ck(7)])
-    op("v", lambda e: e.memset(T.erw[:], 0.0), [], [("erw", 0, 144)])
-    op("v", tt(col(9), col(8), col(3), MUL), [ck(8), ck(3)], [ck(9)])
-    op("v", tt(col(10), col(5), col(3), MUL), [ck(5), ck(3)], [ck(10)])
-    op("v", tt(col(11), col(7), col(3), MUL), [ck(7), ck(3)], [ck(11)])
-    op("v", ts(col(12), kf[:, 2:3], 3.0, col(5), EQ, MUL), [KF, ck(5)], [ck(12)])
-    op("v", ts(T.erw[:, 15:128:16], T.gbd[:, 0:128:16], col(12), None, MUL), [GBD, ck(12)], [("erw", 0, 144)])
-    op("v", ts(T.fa[:], R(4), 0.0, 512.0, EQ, MUL), [RK(4)], [("fa", 0, W)])
-    op("v", ts(T.fra[:], R(1), 10.0, 512.0, EQ, MUL), [RK(1)], [("fra", 0, W)])
-    op("v", ts(T.frb[:], R(1), 11.0, None, EQ), [RK(1)], [("frb", 0, W)])
-    op("v", ts(T.frc[:], R(1), 9.0, 512.0, EQ, MUL), [RK(1)], [("frc", 0, W)])
-    op("v", ts(T.frd[:], R(1), 8.0, 262144.0, EQ, MUL), [RK(1)], [("frd", 0, W)])
-    op("v", ts(T.g11[:], T.gbd[:, 0:W], T.dm[:, 11:12], None, MUL), [GBD, DM], [("g11", 0, W)])
-    op("v", tt(T.idh[:], T.gbd[:, 0:W], T.dm[:], MUL), [GBD, DM], [("idh", 0, W)])
-    op("v", tt(T.fr2[:], T.fra[:], T.frb[:], ADD), [("fra", 0, W), ("frb", 0, W)], [("fr2", 0, W)])
-    op("v", tt(T.fr3[:], T.frc[:], T.frd[:], ADD), [("frc", 0, W), ("frd", 0, W)], [("fr3", 0, W)])
-    op("v", tt(T.r2a[:], T.idh[:], T.fa[:], MUL), [("idh", 0, W), ("fa", 0, W)], [("r2a", 0, W)])
-    op("v", tt(T.r2b[:], T.g11[:], T.fr2[:], MUL), [("g11", 0, W), ("fr2", 0, W)], [("r2b", 0, W)])
-    op("v", tt(T.fr4[:], T.fr2[:], T.fr3[:], ADD), [("fr2", 0, W), ("fr3", 0, W)], [("fr4", 0, W)])
-    op("v", tt(T.r2[:], T.r2a[:], T.r2b[:], ADD), [("r2a", 0, W), ("r2b", 0, W)], [("r2", 0, W)])
-    op("v", tt(T.r4[:], T.g11[:], T.fr4[:], MUL), [("g11", 0, W), ("fr4", 0, W)], [("r4", 0, W)])
-    for t in range(4):
-        op("v", ts(T.gw[:, 136 * t:136 * t + W], T.gbd[:, 96:224], col(10), None, MUL), [GBD, ck(10)], [("gw", 136 * t, 136 * t + W)])
-        op("v", ts(T.gw[:, 136 * t + W:136 * t + 136], T.gbd[:, 32 * t:32 * t + 128:16], col(9), None, MUL), [GBD, ck(9)], [("gw", 136 * t + W, 136 * t + 136)])
-    op("v", ts(T.gl[:, 0:128], T.gbd[:, 96:224], col(10), None, MUL), [GBD, ck(10)], [("gl", 0, 128)])
-    op("v", ts(T.gl[:, 128:256], T.gbd[:, 64:192], col(9), None, MUL), [GBD, ck(9)], [("gl", 128, 256)])
-    op("v", ts(T.gl[:, 256:384], T.gbd[:, 96:224], col(11), None, MUL), [GBD, ck(11)], [("gl", 256, 384)])
-    op("v", ts(T.gl[:, 384:512], T.gbd[:, 96:224], col(9), None, MUL), [GBD, ck(9)], [("gl", 384, 512)])
-    op("v", cp(T.gb8[:], T.gbd[:, 0:128:16]), [GBD], [("gb8", 0, 8)])
     for r in range(16):
-        op("s", act(T.tab[:, r:2048:16], R(5), AF.Identity, bias=T.b16[:, r:r + 1], scale=ro[:, 0:1]),
-           [RK(5), ("b16", 0, 16), ("ro", 0, 1)], [("tab", 0, 2048)])
+        op("s", act(T.tab[:, W * r:W * r + W], T.rm[:], AF.Identity, bias=T.b16[:, r:r + 1], scale=ro[:, 0:1]),
+           [RM, ("b16", 0, 16), ("ro", 0, 1)], [("tab", W * r, W * r + W)])
     for r in range(16):
         op("s", act(T.e16[:, W * r:W * r + W], T.gbd[:, 0:W], AF.Copy, scale=T.d16[:, r:r + 1]),
-           [("gbd", 0, W), ("d16", 0, 16)], [("e16", W * r, W * r + W)])
+           [("gbd", 0, 256), ("d16", 0, 16)], [("e16", W * r, W * r + W)])
 
     nxl = T.landA[:, 0:64, :]
     dma("y", T.s2r[0:32, :], nxl, [("landAn", 0, 1)], [("s2h", 0, 512)], [arrA])
     dma("y", T.s2r[32:64, :], nxl, [("landAn", 0, 1)], [("s2l", 0, 512)], [arrA])
-    dma("s", T.s2r[64:96, :], T.landA[:, 64:128, :], [("landAw", 0, 1)], [("s2w", 0, 512)], [arrA])
-    dma("s", T.l1r[:], nxl, [("landAn", 0, 1)], [("l1r", 0, W)], [arrA])
+    dma("y", T.s2r[64:96, :], T.landA[:, 64:128, :], [("landAw", 0, 1)], [("s2w", 0, 512)], [arrA])
+    for G in range(8):
+        q, y = G // 2, G % 2
+        dma("sy"[y], T.l1r[:, 16 * G:16 * G + 16], T.landA[q, 32 * y:32 * y + 32, :], [("landAn", 0, 1)], [("l1r", 16 * G, 16 * G + 16)], [arrA])
     for t in range(4):
         for r0, r1, sh in ((0, 4 - t, t), (4 - t, 4, t - 4)):
             if r0 < r1:
@@ -289,26 +264,44 @@ def rank_program(g, core, T, topo):
         op("v", ts(T.s2r[0:32, lo:hi], T.s2r[0:32, lo:hi], 127, None, AND), [("s2h", lo, hi)], [("s2h", lo, hi)])
         op("v", cp(T.s2f[0:96, lo:hi], T.s2r[0:96, lo:hi]), [("s2h", lo, hi), ("s2l", lo, hi), ("s2w", lo, hi)], [("s2f", lo, hi)])
         for v in range(4):
-            op("p", mm(T["pb%d" % v][:, lo:hi], T.lbv[:, W * v:W * v + W], T.s2f[:, lo:hi]),
-               [("lbv", W * v, W * v + W), ("s2f", lo, hi), ("s2k", lo, hi)], [("pb%d" % v, 0, 1)])
-    op("v", cp(T.l1[:], T.l1r[:]), [("l1r", 0, W)], [("l1", 0, W)])
-    for v in range(4):
-        lo, hi = 512 * v, 512 * v + 512
-        if v % 2 == 0:
-            op("s", act(T.t0[:, lo:hi], T["pb%d" % v][:]), [("pb%d" % v, 0, 1)], [("t0", lo, hi)])
-        else:
-            op("v", cp(T.t0[:, lo:hi], T["pb%d" % v][:]), [("pb%d" % v, 0, 1)], [("t0", lo, hi)])
-    for v in range(4):
-        op("p", mm(T["pb%d" % (4 + v)][:], T.liv[:, W * v:W * v + W], T.s2f[:]),
-           [("liv", W * v, W * v + W), ("s2f", 0, 512), ("s2k", 0, 512)], [("pb%d" % (4 + v), 0, 1)])
+            b = "pb%d" % (v + 4 * h)
+            op("p", mm(T[b][:, 0:256], T.lbv[0:96, W * v:W * v + W], T.s2f[0:96, lo:hi]),
+               [("lbv", W * v, W * v + W), ("s2f", lo, hi)], [(b, 0, 1)])
 
-    def gather(q, out, okey, lo, hi, win, wkey, w0, lst, lkey):
+    def copy0(q, v, h):
+        b, lo = "pb%d" % (v + 4 * h), 512 * v + 256 * h
+        c = act if q == "s" else cp
+        op(q, c(T.t0[:, lo:lo + 256], T[b][:, 0:256]), [(b, 0, 1)], [("t0", lo, lo + 256)])
+    for q, v, h in (("s", 0, 0), ("s", 1, 0), ("s", 2, 0), ("s", 3, 0), ("v", 0, 1)):
+        copy0(q, v, h)
+    op("v", cp(T.l1f[:], T.l1r[:]), [("l1r", 0, W)], [("l1f", 0, W)])
+    op("p", mm(T.pb0[:, 0:128], T.l1f[:], T.idh[:]), [("l1f", 0, W), ("idh", 0, W)], [("pb0", 0, 1)])
+    copy0("v", 1, 1)
+    copy0("s", 2, 1)
+    copy0("s", 3, 1)
+    op("v", cp(T.l1[:], T.pb0[:, 0:128]), [("pb0", 0, 1)], [("l1", 0, W)])
+    I1 = ["pb1", "pb2", "pb3", "pb0"]
+    for v in range(4):
+        op("p", mm(T[I1[v]][:], T.liv[0:96, W * v:W * v + W], T.s2f[0:96, :]),
+           [("liv", W * v, W * v + W), ("s2f", 0, 512)], [(I1[v], 0, 1)])
+
+    def gather(q, out, okey, lo, hi, win, wkey, w0, lst, lkey, mask=None):
         src = win[:, w0:w0 + 2048].indirect(lst[:, lo // 16:hi // 16])
         rd = [(wkey, w0, w0 + 2048), (lkey, lo // 16, hi // 16)]
+        if mask is not None:
+            rd.append(KF)
         if q == "v":
-            op("v", cp(out[:, lo:hi], src), rd, [(okey, lo, hi)])
+            op("v", cp(out[:, lo:hi], src) if mask is None else ts(out[:, lo:hi], src, mask, None, MUL), rd, [(okey, lo, hi)])
         else:
-            op("s", act(out[:, lo:hi], src), rd, [(okey, lo, hi)])
+            op("s", act(out[:, lo:hi], src) if mask is None else act(out[:, lo:hi], src, scale=mask), rd, [(okey, lo, hi)])
+
+    def fix(dst, dkey, d0, buf, bkey, banks, lo, hi):
+        while lo < hi:
+            c = lo // 512
+            m = min(hi, 512 * c + 512)
+            op("v", tt(dst[:, d0 + lo:d0 + m], buf[:, lo:m], T[banks[c]][:, lo - 512 * c:m - 512 * c], MAX),
+               [(bkey, lo, m), (banks[c], 0, 1)], [(dkey, d0 + lo, d0 + m)])
+            lo = m
 
     def relay(h, pbn, gbuf, gkey):
         for r in range(16):
@@ -318,169 +311,162 @@ def rank_program(g, core, T, topo):
     def relist(h, pbn, lst, lkey):
         op("v", cp(lst[:, 64 * h:64 * h + 64], T[pbn][:, 0:64]), [(pbn, 0, 1)], [(lkey, 64 * h, 64 * h + 64)])
 
-    SPL = [("v", 0, 384), ("s", 384, 1024), ("v", 1024, 1408), ("s", 1408, 2048)]
-    for q, lo, hi in SPL:
-        gather(q, T.ga, "ga", lo, hi, T.t0, "t0", 0, T.l1, "l1")
-    relay(0, "pb0", T.ga, "ga")
-    relay(1, "pb1", T.ga, "ga")
-    for h in range(2):
-        for r in range(16):
-            b = "pb%d" % (4 + r // 4)
-            s = slice(1024 * h + r, 1024 * h + 1024, 16)
-            op("v", tt(T.t1[:, s], T.ga[:, s], T[b][:, (r % 4) * 128 + 64 * h:(r % 4) * 128 + 64 * h + 64], MAX),
-               [("ga", 1024 * h, 1024 * h + 1024), (b, 0, 1)], [("t1", 1024 * h, 1024 * h + 1024)])
-        relist(h, "pb%d" % h, T.l2, "l2")
-    I2 = ["pb2", "pb3", "pb4", "pb5"]
+    gather("v", T.ga, "ga", 0, 384, T.t0, "t0", 0, T.l1, "l1", k(7))
+    for lo, hi in ((384, 512), (512, 1024), (1024, 1536), (1536, 1888), (1888, 2048)):
+        gather("s", T.ga, "ga", lo, hi, T.t0, "t0", 0, T.l1, "l1", k(7))
+    relay(0, "pb4", T.ga, "ga")
+    fix(T.t1, "t1", 0, T.ga, "ga", I1, 0, 512)
+    fix(T.t1, "t1", 0, T.ga, "ga", I1, 512, 1024)
+    for l in range(2):
+        op("v", ts(T.ei[:, 64 * l:64 * l + 64], T.ep[:, l, :], 3, None, ADD), EPK, [("ei", 64 * l, 64 * l + 64)])
+    op("v", ts(T.fi[:], T.ei[:], 3, None, AND), [("ei", 0, W)], [("fi", 0, W)])
+    I2 = ["pb6", "pb7", "pb1", "pb2"]
 
     def in2(c):
         op("p", mm(T[I2[c]][:], T.r2[:], T.t1[:, 512 * c:512 * c + 512]), [("r2", 0, W), ("t1", 512 * c, 512 * c + 512)], [(I2[c], 0, 1)])
-
-    def fix2(c):
-        lo, hi = 512 * c, 512 * c + 512
-        op("v", tt(T.tab[:, 2048 + lo:2048 + hi], T.gb[:, lo:hi], T[I2[c]][:], MAX), [("gb", lo, hi), (I2[c], 0, 1)], [("tab", 2048 + lo, 2048 + hi)])
-    for q, lo, hi in SPL:
-        gather(q, T.gb, "gb", lo, hi, T.t1, "t1", 0, T.l2, "l2")
     in2(0)
+    relay(1, "pb5", T.ga, "ga")
     in2(1)
+    fix(T.t1, "t1", 0, T.ga, "ga", I1, 1024, 1536)
     in2(2)
-    relay(0, "pb0", T.gb, "gb")
+    relist(0, "pb4", T.l2, "l2")
+    fix(T.t1, "t1", 0, T.ga, "ga", I1, 1536, 1888)
+    fix(T.t1, "t1", 0, T.ga, "ga", I1, 1888, 2048)
     in2(3)
-    relay(1, "pb1", T.gb, "gb")
-    fix2(0)
-    fix2(1)
-    for l in range(2):
-        op("v", ts(T.ei[:, 64 * l:64 * l + 64], T.ep[:, l, :], 3, None, ADD), EPK, [("ei", 64 * l, 64 * l + 64)])
-    op("v", ts(T.xa[:], T.xr[:], 127, None, AND), [("xr", 0, 16)], [("xa", 0, 16)])
-    op("v", ts(T.xb[:], T.xr[:], 7, None, SHR), [("xr", 0, 16)], [("xb", 0, 16)])
-    op("v", ts(T.fi[:], T.ei[:], 3, None, AND), [("ei", 0, W)], [("fi", 0, W)])
-    op("v", ts(T.ki[:], T.ei[:], 2, None, SHR), [("ei", 0, W)], [("ki", 0, W)])
-    fix2(2)
-    op("v", ts(T.xc[:], T.xa[:], 16, None, MUL), [("xa", 0, 16)], [("xc", 0, 16)])
-    op("v", cp(T.fb[:], T.fi[:]), [("fi", 0, W)], [("fb", 0, W)])
-    op("v", ts(T.off[:], T.ki[:], 2048, None, MUL), [("ki", 0, W)], [("off", 0, W)])
-    relist(0, "pb0", T.l4, "l4")
-    op("v", tt(T.xd[:], T.xc[:], T.xb[:], ADD), [("xc", 0, 16), ("xb", 0, 16)], [("xd", 0, 16)])
-    fix2(3)
-    relist(1, "pb1", T.l4, "l4")
-    C4 = ["pb6", "pb7", "pb2", "pb3"]
-    for c in range(4):
-        op("p", mm(T[C4[c]][:], T.r4[:], T.tab[:, 2048 + 512 * c:2560 + 512 * c]), [("r4", 0, W), ("tab", 2048 + 512 * c, 2560 + 512 * c)], [(C4[c], 0, 1)])
-    EMB = ["pb0", "pb1", "pb4", "pb5"]
 
-    def em_rows(c):
+    gather("v", T.gb, "gb", 0, 384, T.t1, "t1", 0, T.l2, "l2", k(6))
+    for lo, hi in ((384, 512), (512, 1024)):
+        gather("s", T.gb, "gb", lo, hi, T.t1, "t1", 0, T.l2, "l2", k(6))
+    relist(1, "pb5", T.l2, "l2")
+    fix(T.tab, "tab", 2048, T.gb, "gb", I2, 0, 512)
+    for lo, hi in ((1024, 1536), (1536, 1888), (1888, 2048)):
+        gather("s", T.gb, "gb", lo, hi, T.t1, "t1", 0, T.l2, "l2", k(6))
+    relay(0, "pb4", T.gb, "gb")
+    C4 = ["pb3", "pb0", "pb6", "pb7"]
+
+    def c4(c):
+        op("p", mm(T[C4[c]][:], T.r4[:], T.tab[:, 2048 + 512 * c:2560 + 512 * c]), [("r4", 0, W), ("tab", 2048 + 512 * c, 2560 + 512 * c)], [(C4[c], 0, 1)])
+    op("v", ts(T.ki[:], T.ei[:], 2, None, SHR), [("ei", 0, W)], [("ki", 0, W)])
+    fix(T.tab, "tab", 2048, T.gb, "gb", I2, 512, 1024)
+    op("v", cp(T.fb[:], T.fi[:]), [("fi", 0, W)], [("fb", 0, W)])
+    relay(1, "pb5", T.gb, "gb")
+    fix(T.tab, "tab", 2048, T.gb, "gb", I2, 1024, 1536)
+    fix(T.tab, "tab", 2048, T.gb, "gb", I2, 1536, 1888)
+    relist(0, "pb4", T.l4, "l4")
+    fix(T.tab, "tab", 2048, T.gb, "gb", I2, 1888, 2048)
+    for c in range(4):
+        c4(c)
+    N1, N2 = 576, 640
+    gather("v", T.ga, "ga", 0, 384, T.tab, "tab", 2048, T.l4, "l4")
+    gather("s", T.ga, "ga", N1, 1024, T.tab, "tab", 2048, T.l4, "l4")
+    relist(1, "pb5", T.l4, "l4")
+    gather("v", T.ga, "ga", 384, N1, T.tab, "tab", 2048, T.l4, "l4")
+    for lo, hi in ((1024, 1536), (1536, 1888), (1888, 2048)):
+        gather("s", T.ga, "ga", lo, hi, T.tab, "tab", 2048, T.l4, "l4")
+    EMB = ["pb1", "pb2", "pb4", "pb5"]
+    for c in range(4):
         for r in range(16):
             op("p", mm(T[EMB[c]][:, r:512:16], T.e16[:, W * r:W * r + W], T.fb[:, 32 * c:32 * c + 32]),
                [("e16", W * r, W * r + W), ("fb", 32 * c, 32 * c + 32)], [(EMB[c], 0, 1)])
-
-    def em_sq(c):
-        op("s", act(T.sq[:, 512 * c:512 * c + 512], T[EMB[c]][:], AF.Square, bias=col(14)), [(EMB[c], 0, 1), ck(14)], [("sq", 512 * c, 512 * c + 512)])
-
-    def em_mask(c):
-        op("s", act(T.em[:, 512 * c:512 * c + 512], T.sq[:, 512 * c:512 * c + 512], AF.Relu, bias=1.0, scale=-1.0), [("sq", 512 * c, 512 * c + 512)], [("em", 512 * c, 512 * c + 512)])
-    for c in range(4):
-        em_rows(c)
-
-    def fixb(k, gbuf, gkey, lo, hi):
-        c = lo // 512
-        o = 2048 * k + 2048
-        op("v", tt(T.tab[:, o + lo:o + hi], gbuf[:, lo:hi], T[C4[c]][:, lo - 512 * c:hi - 512 * c], MAX),
-           [(gkey, lo, hi), (C4[c], 0, 1)], [("tab", o + lo, o + hi)])
-    gather("v", T.ga, "ga", 0, 640, T.tab, "tab", 2048, T.l4, "l4")
-    for lo, hi in ((640, 1024), (1024, 1536), (1536, 2048)):
-        gather("s", T.ga, "ga", lo, hi, T.tab, "tab", 2048, T.l4, "l4")
-    for c in range(4):
-        fixb(1, T.ga, "ga", 512 * c, 512 * c + 512)
+    fix(T.tab, "tab", 4096, T.ga, "ga", C4, 0, 1024)
     op("s", act(T.c4a[:, 0:512], T[C4[0]][:]), [(C4[0], 0, 1)], [("c4a", 0, 512)])
-    op("s", act(T.c4a[:, 512:640], T[C4[1]][:, 0:128]), [(C4[1], 0, 1)], [("c4a", 512, 640)])
-    op("v", tt(T.xe[:], T.xd[:], T.off[:, 0:16], ADD), [("xd", 0, 16), ("off", 0, 16)], [("xe", 0, 16)])
-    for k in (2, 3):
-        gbuf, gkey = (T.gb, "gb") if k == 2 else (T.ga, "ga")
-        o = 2048 * k + 2048
-        op("v", tt(T.tab[:, o:o + 640], T.tab[:, o - 2048:o].indirect(T.l4[:, 0:40]), T.c4a[:], MAX),
-           [("tab", o - 2048, o), ("l4", 0, 40), ("c4a", 0, 640)], [("tab", o, o + 640)])
-        for lo, hi in ((1024, 1536), (1536, 2048), (640, 1024)):
+    op("s", act(T.c4a[:, 512:N2], T[C4[1]][:, 0:N2 - 512]), [(C4[1], 0, 1)], [("c4a", 512, N2)])
+    for lo, hi in ((1024, 1536), (1536, 1888), (1888, 2048)):
+        fix(T.tab, "tab", 4096, T.ga, "ga", C4, lo, hi)
+
+    def ecopy(t):
+        lo = 256 * t
+        c = lo // 512
+        op("s", act(T.ec[:, lo:lo + 256], T[EMB[c]][:, lo - 512 * c:lo - 512 * c + 256]), [(EMB[c], 0, 1)], [("ec", lo, lo + 256)])
+
+    def emask(t):
+        lo = 256 * t
+        op("v", ts(T.em[:, lo:lo + 256], T.ec[:, lo:lo + 256], col(7), None, EQ), [("ec", lo, lo + 256), ck(7)], [("em", lo, lo + 256)])
+    for kk in (2, 3):
+        gbuf, gkey = (T.gb, "gb") if kk == 2 else (T.ga, "ga")
+        o = 2048 * kk + 2048
+        op("v", tt(T.tab[:, o:o + N2], T.tab[:, o - 2048:o].indirect(T.l4[:, 0:N2 // 16]), T.c4a[:, 0:N2], MAX),
+           [("tab", o - 2048, o), ("l4", 0, N2 // 16), ("c4a", 0, N2)], [("tab", o, o + N2)])
+        chunks = ((N2, 1024), (1024, 1536), (1536, 1888), (1888, 2048))
+        for lo, hi in chunks:
             gather("s", gbuf, gkey, lo, hi, T.tab, "tab", o - 2048, T.l4, "l4")
-        for lo, hi in ((1024, 1536), (1536, 2048), (640, 1024)):
-            fixb(k, gbuf, gkey, lo, hi)
-        if k == 2:
-            em_sq(0)
-        else:
-            em_mask(0)
-            for c in (1, 2, 3):
-                em_sq(c)
-                em_mask(c)
-    for b in range(2):
-        op("v", cp(T["ql%d" % b][:], T.xe[:, 8 * b:8 * b + 8]), [("xe", 0, 16)], [("ql%d" % b, 0, 8)])
+        if kk == 2:
+            ecopy(0)
+            ecopy(1)
+            op("v", ts(T.off[:], T.ki[:], 2048, None, MUL), [("ki", 0, W)], [("off", 0, W)])
+            op("v", tt(T.xe[:], T.xr[:], T.off[:, 0:16], ADD), [("xr", 0, 16), ("off", 0, 16)], [("xe", 0, 16)])
+            for b in range(2):
+                op("v", cp(T["ql%d" % b][:], T.xe[:, 8 * b:8 * b + 8]), [("xe", 0, 16)], [("ql%d" % b, 0, 8)])
+        for lo, hi in chunks:
+            fix(T.tab, "tab", o, gbuf, gkey, C4, lo, hi)
+            if kk == 3 and lo == 1024:
+                emask(0)
+    for t in range(2, 6):
+        ecopy(t)
 
-    PX, PL = ["pb6", "pb7"], ["pb2", "pb3"]
+    PX, PL, PW, PLW = ["pb3", "pb0"], ["pb6", "pb7"], ["pb1", "pb2"], "pb4"
 
-    def step(t, b):
+    def look(t, b):
         q, x = "ql%d" % b, "x%d" % b
         lo = 256 * t + 128 * b
         op("v", tt(T[x][:], T.tab[:].indirect(T[q][:]), T.em[:, lo:lo + 128], MUL), [("tab", 0, 10240), (q, 0, 8), ("em", lo, lo + 128)], [(x, 0, W)])
-        if t < 6:
-            c = 136 * (t % 4)
-            op("p", mm(T[PX[b]][:, 0:136], T[x][:], T.gw[:, c:c + 136]), [(x, 0, W), ("gw", c, c + 136)], [(PX[b], 0, 1)])
-        else:
-            c = 256 * (t - 6)
-            op("p", mm(T[PX[b]][:, 0:256], T[x][:], T.gl[:, c:c + 256]), [(x, 0, W), ("gl", c, c + 256)], [(PX[b], 0, 1)])
+
+    def sums(t, b):
+        x, y, yw, c, o = "x%d" % b, "y%d" % b, "yw%d" % b, 2 * (t % 4), W * (t % 2)
+        for r in range(16):
+            op("p", mm(T[PX[b]][0:8, r:128:16], T[x][:, r:128:16], T.pc[:, 6:14]), [(x, 0, W), ("pc", 0, 16)], [(PX[b], 0, 1)])
+        op("s", act(T[y][0:8, :], T[PX[b]][0:8, 0:128]), [(PX[b], 0, 1)], [(y, 0, W)])
+        for r in range(16):
+            op("p", mm(T[PW[b]][0:8, r:128:16], T[x][:, r:128:16], T.wc[:, c:c + 8]), [(x, 0, W), ("wc", 0, 16)], [(PW[b], 0, 1)])
+        op("s", act(T[yw][0:8, o:o + W], T[PW[b]][0:8, 0:128]), [(PW[b], 0, 1)], [(yw, o, o + W)])
         if t < 7:
             o = 16 * (t + 1) + 8 * b
             op("p", mm(T[PL[b]][:, 0:8], T.idh[:], T.off[:, o:o + 8], True, False), [("idh", 0, W), ("off", o, o + 8)], [(PL[b], 0, 1)])
 
     def turn(t, b):
-        y = "y%d" % b
-        op("v", tt(T[y][:], T[PX[b]][:, 0:128], T.dm[:], MUL), [(PX[b], 0, 1), DM], [(y, 0, W)])
-        op("p", mm(T[PL[b]][:, 0:8], T[y][:], T.gb8[:], t == 7, True), [(y, 0, W), ("gb8", 0, 8)], [(PL[b], 0, 1)])
-
-    def weigh(t, b):
-        a = T.acc[:, 8 * b:8 * b + 8]
-        if t == 0:
-            op("v", cp(a, T[PX[b]][:, 128:136]), [(PX[b], 0, 1)], [("acc", 8 * b, 8 * b + 8)])
-        elif t < 6:
-            op("v", tt(a, a, T[PX[b]][:, 128:136], MAX), [(PX[b], 0, 1), ("acc", 8 * b, 8 * b + 8)], [("acc", 8 * b, 8 * b + 8)])
+        y, q = "y%d" % b, "ql%d" % b
+        op("p", mm(T[PL[b]][:, 0:8], T[y][0:8, :], T.idh[0:8, 0:8], t == 7, True), [(y, 0, W), ("idh", 0, W)], [(PL[b], 0, 1)])
+        if t < 7:
+            op("v", cp(T[q][:], T[PL[b]][:, 0:8]), [(PL[b], 0, 1)], [(q, 0, 8)])
         else:
-            yw = "yw%d" % b
-            op("v", tt(T[yw][:], T[PX[b]][:, 128:256], T.dm[:], MUL), [(PX[b], 0, 1), DM], [(yw, 0, W)])
-            pw = ("pb0", "pb1")[b]
-            op("p", mm(T[pw][:, 0:8], T[yw][:], T.gbd[:, 0:128:16]), [(yw, 0, W), ("gbd", 0, W)], [(pw, 0, 1)])
+            op("v", cp(T.outb[:, 8 * b:8 * b + 8], T[PL[b]][:, 0:8]), [(PL[b], 0, 1)], [("outb", 8 * b, 8 * b + 8)])
 
-    def relq(b):
-        q = "ql%d" % b
-        op("v", cp(T[q][:], T[PL[b]][:, 0:8]), [(PL[b], 0, 1)], [(q, 0, 8)])
+    def wturn(t, b):
+        yw, o = "yw%d" % b, W * (t % 2)
+        op("p", mm(T[PLW][:, 8 * b:8 * b + 8], T[yw][0:8, o:o + W], T.idh[0:8, 0:8]), [(yw, o, o + W), ("idh", 0, W)], [(PLW, 0, 1)])
 
-    step(0, 0)
-    step(0, 1)
-    for t in range(7):
+    def weigh(t):
+        if t == 0:
+            op("v", cp(T.acc[:], T[PLW][:, 0:16]), [(PLW, 0, 1)], [("acc", 0, 16)])
+        elif t < 7:
+            op("v", tt(T.acc[:], T.acc[:], T[PLW][:, 0:16], MAX), [(PLW, 0, 1), ("acc", 0, 16)], [("acc", 0, 16)])
+        else:
+            op("v", tt(T.outb[:, 16:32], T.acc[:], T[PLW][:, 0:16], MAX), [(PLW, 0, 1), ("acc", 0, 16)], [("outb", 16, 32)])
+
+    look(0, 0)
+    emask(1)
+    for t in range(8):
+        if t > 0:
+            turn(t - 1, 1)
+        sums(t, 0)
+        look(t, 1)
+        if t > 0:
+            wturn(t - 1, 0)
+            wturn(t - 1, 1)
+            weigh(t - 1)
+        if t == 1:
+            ecopy(6)
+            ecopy(7)
         turn(t, 0)
-        turn(t, 1)
-        weigh(t, 0)
-        relq(0)
-        step(t + 1, 0)
-        weigh(t, 1)
-        relq(1)
-        step(t + 1, 1)
-        if t == 5:
-            for r in range(16):
-                op("s", act(T.yp[:, r:256:16], T.acc[:], AF.Copy, scale=T.d16[:, r:r + 1]), [("acc", 0, 16), ("d16", 0, 16)], [("yp", 0, 256)])
-    for b in range(2):
-        pw = ("pb4", "pb5")[b]
-        op("p", mm(T[pw][:, 0:8], T.yp[:, W * b:W * b + W], T.gbd[:, 0:128:16]), [("yp", 0, 256), ("gbd", 0, W)], [(pw, 0, 1)])
-    for b in range(2):
-        s = slice(8 * b, 8 * b + 8)
-        op("v", cp(T.m06[:, s], T[("pb0", "pb1")[b]][:, 0:8]), [(("pb0", "pb1")[b], 0, 1)], [("m06", 8 * b, 8 * b + 8)])
-    turn(7, 0)
-    weigh(7, 0)
+        sums(t, 1)
+        if t < 7:
+            look(t + 1, 0)
+        if t < 6:
+            emask(t + 2)
     turn(7, 1)
-    weigh(7, 1)
-    for b in range(2):
-        s = slice(8 * b, 8 * b + 8)
-        op("v", tt(T.m05[:, s], T.m06[:, s], T[("pb4", "pb5")[b]][:, 0:8], MAX), [("m06", 8 * b, 8 * b + 8), (("pb4", "pb5")[b], 0, 1)], [("m05", 8 * b, 8 * b + 8)])
-    for b in range(2):
-        op("v", cp(T.outb[:, 8 * b:8 * b + 8], T[PL[b]][:, 0:8]), [(PL[b], 0, 1)], [("outb", 8 * b, 8 * b + 8)])
-        s = slice(8 * b, 8 * b + 8)
-        pw = ("pb0", "pb1")[b]
-        op("v", tt(T.outb[:, 16 + 8 * b:24 + 8 * b], T.m05[:, s], T[pw][:, 0:8], MAX), [("m05", 8 * b, 8 * b + 8), (pw, 0, 1)], [("outb", 16 + 8 * b, 24 + 8 * b)])
+    wturn(7, 0)
+    wturn(7, 1)
+    weigh(7)
 
     arrO = send(lambda s: T.outb[:], T.landO[rank], "arrO", "locO", [("outb", 0, 32)])
     dma("y", T.landO[rank], T.outb[:], [("outb", 0, 32)], [("landO", 0, 1)])

import numpy as np
from concourse.bass import DstId, RemoteDMATransfer
from concourse.mybir import dt, AluOpType, ActivationFunctionType

ND = 40
SCRATCH = {
    "srcA": ("dram", [4, 128, 64], "int32"), "srcE": ("dram", [4, 128, 32], "int32"), "srcX": ("dram", [4, 128, 4], "int32"),
    "landA": ("dram", [4, 128, 64], "int32"), "landE": ("dram", [4, 128, 32], "int32"), "landX": ("dram", [4, 128, 4], "int32"),
    "landO": ("dram", [4, 128, 32], "float32"),
    "s2r": ("sbuf", [128, 512], "int32"), "s2f": ("sbuf", [128, 512], "float16"), "l1r": ("sbuf", [128, 128], "int32"), "l1f": ("sbuf", [128, 128], "float16"),
    "ep": ("sbuf", [128, 2, 64], "int32"), "ei": ("sbuf", [128, 128], "int32"), "fi": ("sbuf", [128, 128], "int32"), "ki": ("sbuf", [128, 128], "int32"),
    "fb": ("sbuf", [128, 128], "bfloat16"), "off": ("sbuf", [128, 128], "float16"), "xr": ("sbuf", [128, 16], "int32"), "xe": ("sbuf", [128, 16], "int32"),
    "t0": ("sbuf", [128, 2048], "bfloat16"), "t1": ("sbuf", [128, 2048], "bfloat16"), "tab": ("sbuf", [128, 10240], "bfloat16"),
    "ga": ("sbuf", [128, 2048], "bfloat16"), "gb": ("sbuf", [128, 2048], "bfloat16"), "c4a": ("sbuf", [128, 640], "bfloat16"),
    "l1": ("sbuf", [128, 128], "uint16"), "l2": ("sbuf", [128, 128], "uint16"), "l4": ("sbuf", [128, 128], "uint16"),
    "ec": ("sbuf", [128, 2048], "bfloat16"), "em": ("sbuf", [128, 2048], "bfloat16"),
    "ql0": ("sbuf", [128, 8], "uint16"), "ql1": ("sbuf", [128, 8], "uint16"),
    "x0": ("sbuf", [128, 128], "bfloat16"), "x1": ("sbuf", [128, 128], "bfloat16"),
    "y0": ("sbuf", [128, 128], "float16"), "y1": ("sbuf", [128, 128], "float16"), "yw0": ("sbuf", [128, 256], "float16"), "yw1": ("sbuf", [128, 256], "float16"),
    "acc": ("sbuf", [128, 16], "float32"), "outb": ("sbuf", [128, 32], "float32"),
    "kq": ("sbuf", [128, 9], "int32"), "kc": ("sbuf", [128, 9], "int32"), "kf": ("sbuf", [128, 9], "float32"),
    "rm": ("sbuf", [128, 128], "bfloat16"), "rc": ("sbuf", [128, 128], "bfloat16"), "rg": ("sbuf", [128, 256], "bfloat16"), "rs": ("sbuf", [128, 128], "bfloat16"),
    "one": ("sbuf", [128, 128], "bfloat16"), "sel": ("sbuf", [128, 128], "bfloat16"), "keep": ("sbuf", [128, 128], "bfloat16"),
    "ro": ("sbuf", [128, 3], "float32"), "rb": ("sbuf", [128, 3], "float32"), "mv": ("sbuf", [128, 4], "float32"), "cf": ("sbuf", [128, 24], "float32"),
    "gbd": ("sbuf", [128, 256], "bfloat16"), "d16": ("sbuf", [128, 16], "float32"), "b16": ("sbuf", [128, 16], "float32"),
    "e16": ("sbuf", [128, 2048], "bfloat16"), "erw": ("sbuf", [128, 144], "bfloat16"), "pc": ("sbuf", [128, 16], "bfloat16"), "wc": ("sbuf", [128, 16], "bfloat16"),
    "idh": ("sbuf", [128, 128], "float16"),
    "la": ("sbuf", [128, 128], "bfloat16"), "lc": ("sbuf", [128, 128], "bfloat16"), "lb": ("sbuf", [128, 128], "bfloat16"), "li": ("sbuf", [128, 128], "bfloat16"),
    "lbv": ("sbuf", [128, 512], "float16"), "liv": ("sbuf", [128, 512], "float16"),
    "r2a": ("sbuf", [128, 128], "bfloat16"), "r2b": ("sbuf", [128, 128], "bfloat16"), "r2": ("sbuf", [128, 128], "bfloat16"), "r4": ("sbuf", [128, 128], "bfloat16"),
}
for _i in range(8):
    SCRATCH["pb%d" % _i] = ("psum", [128, 512], "float32")
SEMAPHORES = ["vv", "ss", "pp", "gq", "arrA", "arrE", "arrX", "arrO", "locA", "locE", "locX", "locO"] + ["d%d" % _i for _i in range(ND)]

ADD, SUB, MUL, MAX, EQ = AluOpType.add, AluOpType.subtract, AluOpType.mult, AluOpType.max, AluOpType.is_equal
AND, SHR = AluOpType.bitwise_and, AluOpType.logical_shift_right
AF = ActivationFunctionType


def rank_program(g, core, T, topo):
    rank = T.rank_of(core)
    if rank is None:
        return
    queues = {"v": g.vector, "s": g.scalar, "p": g.tensor, "g": g, "y": g.sync}
    comp = {"v": "vv", "s": "ss", "p": "pp", "g": "gq"}
    total, known, hist, bank, dmas = {}, {q: {} for q in queues}, {}, {}, [0]

    def wait(q, tok):
        sem, val, know = tok
        if known[q].get(sem, 0) < val:
            queues[q].wait_ge(T.sem[sem], val)
            known[q][sem] = val
            for a, b in know.items():
                if known[q].get(a, 0) < b:
                    known[q][a] = b

    def deps(q, reads, writes, is_dma):
        need = []
        for regs, w in ((reads, False), (writes, True)):
            for key, lo, hi in regs:
                if key[:2] == "pb":
                    for oq, tok in bank.get(key, {}).items():
                        if oq != q:
                            need.append(tok)
                    continue
                for l, h, tok, oq, ow in hist.get(key, []):
                    if l < hi and lo < h and (w or ow):
                        same = oq == q and not is_dma
                        if same and w:
                            continue
                        need.append(tok)
        best = {}
        for tok in need:
            if tok[0] not in best or best[tok[0]][1] < tok[1]:
                best[tok[0]] = tok
        toks = list(best.values())
        for tok in toks:
            if any(o is not tok and o[2].get(tok[0], 0) >= tok[1] for o in toks):
                continue
            wait(q, tok)

    def note(q, tok, reads, writes, is_dma):
        for regs, w in ((reads, False), (writes, True)):
            for key, lo, hi in regs:
                if key[:2] == "pb":
                    bank.setdefault(key, {})[q] = tok
                    continue
                old = hist.setdefault(key, [])
                if w:
                    hist[key] = old = [o for o in old if not (lo <= o[0] and o[1] <= hi)]
                old.append((lo, hi, tok, "dma" if is_dma else q, w))

    def op(q, call, reads, writes):
        deps(q, reads, writes, False)
        sem = comp[q]
        total[sem] = total.get(sem, 0) + 1
        tok = (sem, total[sem], dict(known[q]))
        call(queues[q]).then_inc(T.sem[sem], 1)
        note(q, tok, reads, writes, False)
        return tok

    def dma(q, out, in_, reads, writes, extra=()):
        for tok in extra:
            wait(q, tok)
        deps(q, reads, writes, True)
        sem = "d%d" % dmas[0]
        dmas[0] += 1
        total[sem] = 16
        tok = (sem, 16, dict(known[q]))
        queues[q].dma_start(out, in_).then_inc(T.sem[sem], 16)
        note(q, tok, reads, writes, True)
        return tok

    others = [s for s in range(4) if s != rank]
    SHARE = 4

    def send(src_of, dst, arr, loc, reads):
        deps("g", reads, [], True)
        tr = []
        for i, s in enumerate(others):
            dstc = T.cores[s]
            a = topo.addr(dstc)
            eng = topo.engines(core, dstc)[SHARE * i:SHARE * (i + 1)]
            tr.append(RemoteDMATransfer(dst_ids=[DstId(rid=a[0], pnc=a[1])], dma_engine_mask=sum(1 << k for k in eng),
                                        remote_sem=T.sem[arr], src=src_of(s), dst=dst))
        g.remote_dma_fused(tr, local_sem=T.sem[loc])
        total[loc] = 3 * SHARE
        total[arr] = 3 * SHARE
        return (arr, 3 * SHARE, {})

    def ts(out, in0, s1, s2, *ops):
        return lambda e: e.tensor_scalar(out, in0, s1, s2, *ops)

    def tt(out, in0, in1, o):
        return lambda e: e.tensor_tensor(out, in0, in1, o)

    def cp(out, in_):
        return lambda e: e.tensor_copy(out, in_)

    def act(out, in_, func=AF.Copy, **kw):
        return lambda e: e.activation(out, in_, func, **kw)

    def mm(out, lhsT, rhs, start=True, stop=True):
        return lambda e: e.matmul(out, lhsT, rhs, start, stop)

    def iota(out, pattern, base=0):
        return lambda e: e.iota(out, pattern, base, 0, allow_small_or_imprecise_dtypes=True)

    def asel(out, in_, pattern, cmp_, fill, base):
        return lambda e: e.affine_select(out, in_, pattern, cmp_, fill, base, 0)
    W = 128

    A3, E3, X3 = T.srcA, T.srcE, T.srcX
    dma("y", A3[:, 0:64, :], T.nx[:], [], [("srcAn", 0, 1)])
    dma("s", A3[:, 64:128, :], T.w[:], [], [("srcAw", 0, 1)])
    dma("y", E3[:], T.e[:], [], [("srcE", 0, 1)])
    dma("s", X3[:], T.x[:], [], [("srcX", 0, 1)])
    own = slice(2 * rank, 2 * rank + 2)
    rows = slice(32 * rank, 32 * rank + 32)
    dma("y", T.landA[rank, 0:64, :], T.nx[own, :], [], [("landAn", 0, 1)])
    dma("s", T.landA[rank, 64:128, :], T.w[own, :], [], [("landAw", 0, 1)])
    dma("y", T.landE[rank], T.e[rows, :], [], [("landE", 0, 1)])
    dma("s", T.landX[rank], T.x[rows, :], [], [("landX", 0, 1)])

    op("g", lambda e: e.iota(T.kq[:], [[0, 9]], 0, 1), [], [("kq", 0, 9)])
    op("g", iota(T.rm[:], [[1, 128]]), [], [("rm", 0, W)])
    op("g", iota(T.rg[:], [[0, 2], [1, 8], [0, 16]]), [], [("rg", 0, 256)])
    op("g", iota(T.rc[:], [[1, 32], [0, 4]]), [], [("rc", 0, W)])
    arrA = send(lambda s: A3[s], T.landA[rank], "arrA", "locA", [("srcAn", 0, 1), ("srcAw", 0, 1)])
    op("g", asel(T.rs[:], T.rc[:], [[0, 32], [1, 4]], AluOpType.is_gt, -1.0, 0), [("rc", 0, W)], [("rs", 0, W)])
    op("g", iota(T.one[:], [[0, 128]], 1), [], [("one", 0, W)])
    op("g", asel(T.sel[:], T.one[:], [[0, 32], [-1, 4]], AluOpType.is_gt, 0.0, 2), [("one", 0, W)], [("sel", 0, W)])
    op("g", asel(T.keep[:], T.sel[:], [[0, 8], [1, 4], [0, 4]], AluOpType.not_equal, 1.0, -2), [("sel", 0, W)], [("keep", 0, W)])
    arrE = send(lambda s: E3[s], T.landE[rank], "arrE", "locE", [("srcE", 0, 1)])
    arrX = send(lambda s: X3[s], T.landX[rank], "arrX", "locX", [("srcX", 0, 1)])

    kf, ro, rb, mv, cf = T.kf, T.ro, T.rb, T.mv, T.cf
    for i, (o1, a1, o2, a2) in enumerate([(SHR, 4, None, 0), (AND, 15, None, 0), (AND, 3, None, 0), (SHR, 2, AND, 3),
                                          (SHR, 5, None, 0), (SHR, 2, AND, 7), (AND, 1, None, 0), (SHR, 1, AND, 1), (AND, 127, None, 0)]):
        c = ts(T.kc[:, i:i + 1], T.kq[:, i:i + 1], a1, None, o1) if o2 is None else ts(T.kc[:, i:i + 1], T.kq[:, i:i + 1], a1, a2, o1, o2)
        op("v", c, [("kq", 0, 9)], [("kc", i, i + 1)])
    op("v", cp(kf[:], T.kc[:]), [("kc", 0, 9)], [("kf", 0, 9)])
    KF, RM, RC = ("kf", 0, 9), ("rm", 0, W), ("rc", 0, W)

    def k(i):
        return kf[:, i:i + 1]

    def col(i):
        return cf[:, i:i + 1]

    def ck(i):
        return ("cf", i, i + 1)

    def cts(i, in0, s1, s2, ops, reads):
        op("v", ts(col(i), in0, s1, s2, *ops), reads, [ck(i)])
    for j in range(3):
        op("v", ts(ro[:, j:j + 1], k(3), float(j), None, EQ), [KF], [("ro", j, j + 1)])
    op("v", ts(T.d16[:], T.rm[:, 0:16], k(1), None, EQ), [RM, KF], [("d16", 0, 16)])
    op("v", ts(T.b16[:], T.rm[:, 0:16], ro[:, 1:2], None, MUL), [RM, ("ro", 1, 2)], [("b16", 0, 16)])
    op("v", ts(T.gbd[:], T.rg[:], k(0), None, EQ), [("rg", 0, 256), KF], [("gbd", 0, 256)])
    for j in range(3):
        op("v", ts(rb[:, j:j + 1], k(4), float(j), None, EQ), [KF], [("rb", j, j + 1)])
    for j in range(4):
        op("v", ts(mv[:, j:j + 1], k(2), float(j), None, EQ), [KF], [("mv", j, j + 1)])
    cts(0, rb[:, 1:2], 0.0078125, rb[:, 0:1], (MUL, ADD), [("rb", 0, 2)])
    cts(1, k(5), 4.0, k(4), (MUL, ADD), [KF])
    cts(2, k(5), 4.0, 1.0, (MUL, ADD), [KF])
    cts(3, rb[:, 0:1], -0.0078125, None, (MUL,), [("rb", 0, 1)])
    cts(4, rb[:, 2:3], 1.0, col(0), (MUL, ADD), [("rb", 2, 3), ck(0)])
    cts(5, ro[:, 1:2], 128.0, ro[:, 0:1], (MUL, ADD), [("ro", 0, 2)])
    op("v", ts(T.lc[:], T.rc[:], col(2), col(3), EQ, MUL), [RC, ck(2), ck(3)], [("lc", 0, W)])
    op("v", ts(T.la[:], T.rc[:], col(1), col(4), EQ, MUL), [RC, ck(1), ck(4)], [("la", 0, W)])
    cts(6, k(2), 3.0, col(5), (EQ, MUL), [KF, ck(5)])
    op("v", lambda e: e.memset(T.erw[:], 0.0), [], [("erw", 0, 144)])
    op("v", tt(T.lb[:], T.la[:], T.lc[:], ADD), [("la", 0, W), ("lc", 0, W)], [("lb", 0, W)])
    op("v", ts(T.idh[:], T.rm[:], k(8), None, EQ), [RM, KF], [("idh", 0, W)])
    for v in range(4):
        op("v", ts(T.lbv[:, W * v:W * v + W], T.lb[:], mv[:, v:v + 1], None, MUL), [("lb", 0, W), ("mv", v, v + 1)], [("lbv", W * v, W * v + W)])
    op("v", ts(T.erw[:, 15:128:16], T.gbd[:, 0:128:16], col(6), None, MUL), [("gbd", 0, 256), ck(6)], [("erw", 0, 144)])
    op("v", ts(T.pc[:], T.gbd[:, 0:256:16], col(5), None, MUL), [("gbd", 0, 256), ck(5)], [("pc", 0, 16)])
    op("v", ts(T.wc[:], T.gbd[:, 0:256:16], ro[:, 2:3], None, MUL), [("gbd", 0, 256), ("ro", 2, 3)], [("wc", 0, 16)])
    cts(7, k(6), 2.0, k(7), (MUL, ADD), [KF])
    cts(8, k(0), 4.0, 7.0, (MUL, ADD), [KF])
    cts(9, k(1), 10.0, None, (EQ,), [KF])
    cts(10, k(1), 11.0, None, (EQ,), [KF])
    cts(11, k(6), -1.0, 1.0, (MUL, ADD), [KF])
    cts(12, k(8), 1.0, None, (ADD,), [KF])
    cts(13, col(8), col(9), -5.0, (MUL, ADD), [ck(8), ck(9)])
    cts(14, col(8), col(10), -5.0, (MUL, ADD), [ck(8), ck(10)])
    cts(15, col(9), -1.0, col(11), (MUL, ADD), [ck(9), ck(11)])
    cts(16, col(12), col(15), -1.0, (MUL, ADD), [ck(12), ck(15)])
    op("v", ts(T.r4[:], T.rc[:], col(14), None, EQ), [RC, ck(14)], [("r4", 0, W)])
    op("v", ts(T.r2a[:], T.rm[:], col(16), None, EQ), [RM, ck(16)], [("r2a", 0, W)])
    op("v", ts(T.r2b[:], T.rs[:], col(13), None, EQ), [("rs", 0, W), ck(13)], [("r2b", 0, W)])
    op("v", tt(T.r2[:], T.r2a[:], T.r2b[:], ADD), [("r2a", 0, W), ("r2b", 0, W)], [("r2", 0, W)])
    op("v", tt(T.li[:], T.lb[:], T.keep[:], MUL), [("lb", 0, W), ("keep", 0, W)], [("li", 0, W)])
    for v in range(4):
        op("v", ts(T.liv[:, W * v:W * v + W], T.li[:], mv[:, v:v + 1], None, MUL), [("li", 0, W), ("mv", v, v + 1)], [("liv", W * v, W * v + W)])
    for r in range(16):
        op("s", act(T.tab[:, W * r:W * r + W], T.rm[:], AF.Identity, bias=T.b16[:, r:r + 1], scale=ro[:, 0:1]),
           [RM, ("b16", 0, 16), ("ro", 0, 1)], [("tab", W * r, W * r + W)])
    for r in range(16):
        op("s", act(T.e16[:, W * r:W * r + W], T.gbd[:, 0:W], AF.Copy, scale=T.d16[:, r:r + 1]),
           [("gbd", 0, 256), ("d16", 0, 16)], [("e16", W * r, W * r + W)])

    nxl = T.landA[:, 0:64, :]
    dma("y", T.s2r[0:32, :], nxl, [("landAn", 0, 1)], [("s2h", 0, 512)], [arrA])
    dma("y", T.s2r[32:64, :], nxl, [("landAn", 0, 1)], [("s2l", 0, 512)], [arrA])
    dma("y", T.s2r[64:96, :], T.landA[:, 64:128, :], [("landAw", 0, 1)], [("s2w", 0, 512)], [arrA])
    for G in range(8):
        q, y = G // 2, G % 2
        dma("sy"[y], T.l1r[:, 16 * G:16 * G + 16], T.landA[q, 32 * y:32 * y + 32, :], [("landAn", 0, 1)], [("l1r", 16 * G, 16 * G + 16)], [arrA])
    for t in range(4):
        for r0, r1, sh in ((0, 4 - t, t), (4 - t, 4, t - 4)):
            if r0 < r1:
                dma("y", T.ep[32 * (r0 + sh):32 * (r1 + sh), :, 16 * t:16 * t + 16],
                    T.landE[r0:r1, t // 2::2, 16 * (t % 2):16 * (t % 2) + 16], [("landE", 0, 1)], [("ep%d%d" % (t, r0), 0, 1)], [arrE])
    dma("y", T.xr[:], T.landX[:], [("landX", 0, 1)], [("xr", 0, 16)], [arrX])
    EPK = [("ep%d%d" % (t, r0), 0, 1) for t in range(4) for r0 in (0, 4 - t) if r0 < 4]

    for h in range(2):
        lo, hi = 256 * h, 256 * h + 256
        op("v", ts(T.s2r[0:32, lo:hi], T.s2r[0:32, lo:hi], 127, None, AND), [("s2h", lo, hi)], [("s2h", lo, hi)])
        op("v", cp(T.s2f[0:96, lo:hi], T.s2r[0:96, lo:hi]), [("s2h", lo, hi), ("s2l", lo, hi), ("s2w", lo, hi)], [("s2f", lo, hi)])
        for v in range(4):
            b = "pb%d" % (v + 4 * h)
            op("p", mm(T[b][:, 0:256], T.lbv[0:96, W * v:W * v + W], T.s2f[0:96, lo:hi]),
               [("lbv", W * v, W * v + W), ("s2f", lo, hi)], [(b, 0, 1)])

    def copy0(q, v, h):
        b, lo = "pb%d" % (v + 4 * h), 512 * v + 256 * h
        c = act if q == "s" else cp
        op(q, c(T.t0[:, lo:lo + 256], T[b][:, 0:256]), [(b, 0, 1)], [("t0", lo, lo + 256)])
    for q, v, h in (("s", 0, 0), ("s", 1, 0), ("s", 2, 0), ("s", 3, 0), ("v", 0, 1)):
        copy0(q, v, h)
    op("v", cp(T.l1f[:], T.l1r[:]), [("l1r", 0, W)], [("l1f", 0, W)])
    op("p", mm(T.pb0[:, 0:128], T.l1f[:], T.idh[:]), [("l1f", 0, W), ("idh", 0, W)], [("pb0", 0, 1)])
    copy0("v", 1, 1)
    copy0("s", 2, 1)
    copy0("s", 3, 1)
    op("v", cp(T.l1[:], T.pb0[:, 0:128]), [("pb0", 0, 1)], [("l1", 0, W)])
    I1 = ["pb1", "pb2", "pb3", "pb0"]
    for v in range(4):
        op("p", mm(T[I1[v]][:], T.liv[0:96, W * v:W * v + W], T.s2f[0:96, :]),
           [("liv", W * v, W * v + W), ("s2f", 0, 512)], [(I1[v], 0, 1)])

    def gather(q, out, okey, lo, hi, win, wkey, w0, lst, lkey, mask=None):
        src = win[:, w0:w0 + 2048].indirect(lst[:, lo // 16:hi // 16])
        rd = [(wkey, w0, w0 + 2048), (lkey, lo // 16, hi // 16)]
        if mask is not None:
            rd.append(KF)
        if q == "v":
            op("v", cp(out[:, lo:hi], src) if mask is None else ts(out[:, lo:hi], src, mask, None, MUL), rd, [(okey, lo, hi)])
        else:
            op("s", act(out[:, lo:hi], src) if mask is None else act(out[:, lo:hi], src, scale=mask), rd, [(okey, lo, hi)])

    def fix(dst, dkey, d0, buf, bkey, banks, lo, hi):
        while lo < hi:
            c = lo // 512
            m = min(hi, 512 * c + 512)
            op("v", tt(dst[:, d0 + lo:d0 + m], buf[:, lo:m], T[banks[c]][:, lo - 512 * c:m - 512 * c], MAX),
               [(bkey, lo, m), (banks[c], 0, 1)], [(dkey, d0 + lo, d0 + m)])
            lo = m

    def relay(h, pbn, gbuf, gkey):
        for r in range(16):
            op("p", mm(T[pbn][:, 0:64], T.erw[:, 15 - r:143 - r], gbuf[:, 1024 * h + r:1024 * h + 1024:16], r == 0, r == 15),
               [("erw", 0, 144), (gkey, 1024 * h, 1024 * h + 1024)], [(pbn, 0, 1)])

    def relist(h, pbn, lst, lkey):
        op("v", cp(lst[:, 64 * h:64 * h + 64], T[pbn][:, 0:64]), [(pbn, 0, 1)], [(lkey, 64 * h, 64 * h + 64)])

    gather("v", T.ga, "ga", 0, 384, T.t0, "t0", 0, T.l1, "l1", k(7))
    for lo, hi in ((384, 512), (512, 1024), (1024, 1536), (1536, 1888), (1888, 2048)):
        gather("s", T.ga, "ga", lo, hi, T.t0, "t0", 0, T.l1, "l1", k(7))
    relay(0, "pb4", T.ga, "ga")
    fix(T.t1, "t1", 0, T.ga, "ga", I1, 0, 512)
    fix(T.t1, "t1", 0, T.ga, "ga", I1, 512, 1024)
    for l in range(2):
        op("v", ts(T.ei[:, 64 * l:64 * l + 64], T.ep[:, l, :], 3, None, ADD), EPK, [("ei", 64 * l, 64 * l + 64)])
    op("v", ts(T.fi[:], T.ei[:], 3, None, AND), [("ei", 0, W)], [("fi", 0, W)])
    I2 = ["pb6", "pb7", "pb1", "pb2"]

    def in2(c):
        op("p", mm(T[I2[c]][:], T.r2[:], T.t1[:, 512 * c:512 * c + 512]), [("r2", 0, W), ("t1", 512 * c, 512 * c + 512)], [(I2[c], 0, 1)])
    in2(0)
    relay(1, "pb5", T.ga, "ga")
    in2(1)
    fix(T.t1, "t1", 0, T.ga, "ga", I1, 1024, 1536)
    in2(2)
    relist(0, "pb4", T.l2, "l2")
    fix(T.t1, "t1", 0, T.ga, "ga", I1, 1536, 1888)
    fix(T.t1, "t1", 0, T.ga, "ga", I1, 1888, 2048)
    in2(3)

    gather("v", T.gb, "gb", 0, 384, T.t1, "t1", 0, T.l2, "l2", k(6))
    for lo, hi in ((384, 512), (512, 1024)):
        gather("s", T.gb, "gb", lo, hi, T.t1, "t1", 0, T.l2, "l2", k(6))
    relist(1, "pb5", T.l2, "l2")
    fix(T.tab, "tab", 2048, T.gb, "gb", I2, 0, 512)
    for lo, hi in ((1024, 1536), (1536, 1888), (1888, 2048)):
        gather("s", T.gb, "gb", lo, hi, T.t1, "t1", 0, T.l2, "l2", k(6))
    relay(0, "pb4", T.gb, "gb")
    C4 = ["pb3", "pb0", "pb6", "pb7"]

    def c4(c):
        op("p", mm(T[C4[c]][:], T.r4[:], T.tab[:, 2048 + 512 * c:2560 + 512 * c]), [("r4", 0, W), ("tab", 2048 + 512 * c, 2560 + 512 * c)], [(C4[c], 0, 1)])
    op("v", ts(T.ki[:], T.ei[:], 2, None, SHR), [("ei", 0, W)], [("ki", 0, W)])
    fix(T.tab, "tab", 2048, T.gb, "gb", I2, 512, 1024)
    op("v", cp(T.fb[:], T.fi[:]), [("fi", 0, W)], [("fb", 0, W)])
    relay(1, "pb5", T.gb, "gb")
    fix(T.tab, "tab", 2048, T.gb, "gb", I2, 1024, 1536)
    fix(T.tab, "tab", 2048, T.gb, "gb", I2, 1536, 1888)
    relist(0, "pb4", T.l4, "l4")
    fix(T.tab, "tab", 2048, T.gb, "gb", I2, 1888, 2048)
    for c in range(4):
        c4(c)
    N1, N2 = 576, 640
    gather("v", T.ga, "ga", 0, 384, T.tab, "tab", 2048, T.l4, "l4")
    gather("s", T.ga, "ga", N1, 1024, T.tab, "tab", 2048, T.l4, "l4")
    relist(1, "pb5", T.l4, "l4")
    gather("v", T.ga, "ga", 384, N1, T.tab, "tab", 2048, T.l4, "l4")
    for lo, hi in ((1024, 1536), (1536, 1888), (1888, 2048)):
        gather("s", T.ga, "ga", lo, hi, T.tab, "tab", 2048, T.l4, "l4")
    EMB = ["pb1", "pb2", "pb4", "pb5"]
    for c in range(4):
        for r in range(16):
            op("p", mm(T[EMB[c]][:, r:512:16], T.e16[:, W * r:W * r + W], T.fb[:, 32 * c:32 * c + 32]),
               [("e16", W * r, W * r + W), ("fb", 32 * c, 32 * c + 32)], [(EMB[c], 0, 1)])
    fix(T.tab, "tab", 4096, T.ga, "ga", C4, 0, 1024)
    op("s", act(T.c4a[:, 0:512], T[C4[0]][:]), [(C4[0], 0, 1)], [("c4a", 0, 512)])
    op("s", act(T.c4a[:, 512:N2], T[C4[1]][:, 0:N2 - 512]), [(C4[1], 0, 1)], [("c4a", 512, N2)])
    for lo, hi in ((1024, 1536), (1536, 1888), (1888, 2048)):
        fix(T.tab, "tab", 4096, T.ga, "ga", C4, lo, hi)

    def ecopy(t):
        lo = 256 * t
        c = lo // 512
        op("s", act(T.ec[:, lo:lo + 256], T[EMB[c]][:, lo - 512 * c:lo - 512 * c + 256]), [(EMB[c], 0, 1)], [("ec", lo, lo + 256)])

    def emask(t):
        lo = 256 * t
        op("v", ts(T.em[:, lo:lo + 256], T.ec[:, lo:lo + 256], col(7), None, EQ), [("ec", lo, lo + 256), ck(7)], [("em", lo, lo + 256)])
    for kk in (2, 3):
        gbuf, gkey = (T.gb, "gb") if kk == 2 else (T.ga, "ga")
        o = 2048 * kk + 2048
        op("v", tt(T.tab[:, o:o + N2], T.tab[:, o - 2048:o].indirect(T.l4[:, 0:N2 // 16]), T.c4a[:, 0:N2], MAX),
           [("tab", o - 2048, o), ("l4", 0, N2 // 16), ("c4a", 0, N2)], [("tab", o, o + N2)])
        chunks = ((N2, 1024), (1024, 1536), (1536, 1888), (1888, 2048))
        for lo, hi in chunks:
            gather("s", gbuf, gkey, lo, hi, T.tab, "tab", o - 2048, T.l4, "l4")
        if kk == 2:
            ecopy(0)
            ecopy(1)
            op("v", ts(T.off[:], T.ki[:], 2048, None, MUL), [("ki", 0, W)], [("off", 0, W)])
            op("v", tt(T.xe[:], T.xr[:], T.off[:, 0:16], ADD), [("xr", 0, 16), ("off", 0, 16)], [("xe", 0, 16)])
            for b in range(2):
                op("v", cp(T["ql%d" % b][:], T.xe[:, 8 * b:8 * b + 8]), [("xe", 0, 16)], [("ql%d" % b, 0, 8)])
        for lo, hi in chunks:
            fix(T.tab, "tab", o, gbuf, gkey, C4, lo, hi)
            if kk == 3 and lo == 1024:
                emask(0)
    for t in range(2, 6):
        ecopy(t)

    PX, PL, PW, PLW = ["pb3", "pb0"], ["pb6", "pb7"], ["pb1", "pb2"], "pb4"

    def look(t, b):
        q, x = "ql%d" % b, "x%d" % b
        lo = 256 * t + 128 * b
        op("v", tt(T[x][:], T.tab[:].indirect(T[q][:]), T.em[:, lo:lo + 128], MUL), [("tab", 0, 10240), (q, 0, 8), ("em", lo, lo + 128)], [(x, 0, W)])

    def sums(t, b):
        x, y, yw, c, o = "x%d" % b, "y%d" % b, "yw%d" % b, 2 * (t % 4), W * (t % 2)
        for r in range(16):
            op("p", mm(T[PX[b]][0:8, r:128:16], T[x][:, r:128:16], T.pc[:, 6:14]), [(x, 0, W), ("pc", 0, 16)], [(PX[b], 0, 1)])
        op("s", act(T[y][0:8, :], T[PX[b]][0:8, 0:128]), [(PX[b], 0, 1)], [(y, 0, W)])
        for r in range(16):
            op("p", mm(T[PW[b]][0:8, r:128:16], T[x][:, r:128:16], T.wc[:, c:c + 8]), [(x, 0, W), ("wc", 0, 16)], [(PW[b], 0, 1)])
        op("s", act(T[yw][0:8, o:o + W], T[PW[b]][0:8, 0:128]), [(PW[b], 0, 1)], [(yw, o, o + W)])
        if t < 7:
            o = 16 * (t + 1) + 8 * b
            op("p", mm(T[PL[b]][:, 0:8], T.idh[:], T.off[:, o:o + 8], True, False), [("idh", 0, W), ("off", o, o + 8)], [(PL[b], 0, 1)])

    def turn(t, b):
        y, q = "y%d" % b, "ql%d" % b
        op("p", mm(T[PL[b]][:, 0:8], T[y][0:8, :], T.idh[0:8, 0:8], t == 7, True), [(y, 0, W), ("idh", 0, W)], [(PL[b], 0, 1)])
        if t < 7:
            op("v", cp(T[q][:], T[PL[b]][:, 0:8]), [(PL[b], 0, 1)], [(q, 0, 8)])
        else:
            op("v", cp(T.outb[:, 8 * b:8 * b + 8], T[PL[b]][:, 0:8]), [(PL[b], 0, 1)], [("outb", 8 * b, 8 * b + 8)])

    def wturn(t, b):
        yw, o = "yw%d" % b, W * (t % 2)
        op("p", mm(T[PLW][:, 8 * b:8 * b + 8], T[yw][0:8, o:o + W], T.idh[0:8, 0:8]), [(yw, o, o + W), ("idh", 0, W)], [(PLW, 0, 1)])

    def weigh(t):
        if t == 0:
            op("v", cp(T.acc[:], T[PLW][:, 0:16]), [(PLW, 0, 1)], [("acc", 0, 16)])
        elif t < 7:
            op("v", tt(T.acc[:], T.acc[:], T[PLW][:, 0:16], MAX), [(PLW, 0, 1), ("acc", 0, 16)], [("acc", 0, 16)])
        else:
            op("v", tt(T.outb[:, 16:32], T.acc[:], T[PLW][:, 0:16], MAX), [(PLW, 0, 1), ("acc", 0, 16)], [("outb", 16, 32)])

    look(0, 0)
    emask(1)
    for t in range(8):
        if t > 0:
            turn(t - 1, 1)
        sums(t, 0)
        look(t, 1)
        if t > 0:
            wturn(t - 1, 0)
            wturn(t - 1, 1)
            weigh(t - 1)
        if t == 1:
            ecopy(6)
            ecopy(7)
        turn(t, 0)
        sums(t, 1)
        if t < 7:
            look(t + 1, 0)
        if t < 6:
            emask(t + 2)
    turn(7, 1)
    wturn(7, 0)
    wturn(7, 1)
    weigh(7)

    arrO = send(lambda s: T.outb[:], T.landO[rank], "arrO", "locO", [("outb", 0, 32)])
    dma("y", T.landO[rank], T.outb[:], [("outb", 0, 32)], [("landO", 0, 1)])
    dma("y", T.last[:], T.landO[:, rows, 0:16], [("landO", 0, 1)], [], [arrO])
    dma("s", T.peak[:], T.landO[:, rows, 16:32], [("landO", 0, 1)], [], [arrO])
    for sem, val in total.items():
        if known["g"].get(sem, 0) < val:
            g.wait_ge(T.sem[sem], val)
